import numpy as np, ml_dtypes
CORES = [36,164,52,180,100,228,116,244]
N = 8
import mx_ref
BF = ml_dtypes.bfloat16
def cut(t, i, w=512):
    return t[:, w * i:w * i + w]
def pick(q, e):
    c = np.concatenate([q[0].reshape(128, -1, 4), np.zeros((128, 1, 4), np.uint8)], axis=1); s = np.concatenate([q[1], np.ones((16, 1), np.uint8)], axis=1)
    return (np.ascontiguousarray(c[:, e].reshape(128, -1)), np.ascontiguousarray(s[:, e]))
def join(*qs):
    return (np.concatenate([q[0] for q in qs], axis=1), np.concatenate([q[1] for q in qs], axis=1))
def put(q, e, v):
    c, s = q[0].reshape(128, -1, 4).copy(), q[1].copy(); c[:, e] = v[0].reshape(128, -1, 4); s[:, e] = v[1]
    return (c.reshape(128, -1), s)
def pk(c, s):
    return (np.ascontiguousarray(c), mx_ref.live(s))
def emit(q):
    return q[0], q[1]
def decode(q):
    o = []
    for b in range(4):
        e = np.zeros((128, 128, 4), np.float32); e[np.arange(128), np.arange(128), b] = 1
        o.append(mx_ref.matmul(mx_ref.quantize(e.reshape(128, 512).astype(BF)), q))
    return np.stack(o, axis=2).reshape(128, -1)
def f(rng, *shape):
    return mx_ref.flush((rng.standard_normal(shape, dtype=np.float32) * np.exp2(rng.integers(-2, 3, shape[:-1] + (1,)))).astype(BF))
def wide(rng, *shape, cols=0):
    v = rng.standard_normal(shape, dtype=np.float32) * np.exp2(rng.integers(-12, 13, shape)).astype(np.float32)
    if cols: v *= np.repeat(np.exp2(rng.integers(-cols, cols + 1, shape[:-2] + (1, shape[-1] // 4))) * (rng.random(shape[:-2] + (1, shape[-1] // 4)) > 0.0625), 4, axis=-1).astype(np.float32)
    return mx_ref.flush(v.astype(BF))
P, K, O = 128, 32, 1
def places(t, j):
    return (j + t * np.arange(N)[:, None]) % P
def checks(tab, u):
    return np.stack([mx_ref.matmul(mx_ref.quantize(np.ascontiguousarray(u[r])), tab[r])[:2] for r in range(N)], axis=1)
def judge(c, g, t):
    j = np.arange(P)
    p = (j + t) % N
    at = places(t, j)
    c, a = c[np.arange(N)[:, None], at], np.abs(g[np.arange(N)[:, None], at])
    s = c[p, j]
    for r in range(N):
        s = np.where(p == r, s, s - c[r])
    bad = np.argsort(-np.abs(s), kind="stable")[:K]
    a[p, j] = -1
    return bad, np.argmax(a, axis=0)[bad]
def rebuilt(tab, bad, lost, t):
    at = places(t, bad)
    v = decode(join(*[pick(tab[r], at[r]) for r in range(N)])).reshape(128, N, K, 4)
    new = np.zeros((128, K, 4), np.float32)
    for k in range(K):
        p = (bad[k] + t) % N
        x = v[:, p, k]
        for r in range(N):
            if r != p and r != lost[k]: x = x - v[:, r, k]
        new[:, k] = x
    return mx_ref.quantize(np.ascontiguousarray(new.reshape(128, -1).astype(BF)))
def data(rng):
    return f(rng, N, 128, 4 * P).astype(np.float32).reshape(N, 128, P, 4)
def striped(v):
    v = v.copy()
    for r in range(N):
        j = np.arange(r, P, N)
        v[r][:, j] = 0
        v[r][:, j] = np.sum(v[:, :, j], axis=0)
    return v
def harm(rng, v, stripes, size):
    for j in stripes:
        v[(j + rng.integers(1, N)) % N][:, j] = size * rng.standard_normal((128, 4))
def queries(rng):
    q = np.array(f(rng, 1, 128, 512))
    q[:, :, 8:] = 0
    return np.concatenate([q] * N)
def draw(rng, v, q=None):
    v = v.astype(np.float32).reshape(N, 128, 4 * P)
    v[np.abs(v) < np.float32(2.0 ** -16)] = 0
    return {"tb": v.astype(BF), "u": queries(rng) if q is None else q, "w": f(rng, N, 128, 512 * O)}
def setup_inputs(rng):
    v = striped(data(rng))
    harm(rng, v, rng.permutation(P)[:K + 6], 8)
    return draw(rng, v)
def setup_inputs_again(rng):
    v, q = striped(data(rng) * np.float32(2.0 ** -8)), queries(rng)
    s = np.where(q[0, :, 4:8].astype(np.float32) < 0, -1.0, 1.0)
    q[:, :, :4] = (np.abs(q[:, :, :4].astype(np.float32)) * s).astype(BF)
    q[:, :32, :4] = 0
    on = (np.arange(128) < 32)[:, None]
    at = N * rng.permutation(P // N)[:K // 2] + 2 * rng.integers(0, N // 2, K // 2) + np.arange(K // 2) % 2
    for j in at:
        p = int(j) % N
        m = (p + int(rng.integers(1, N))) % N
        if p % 2:
            m = ((p + 1) // 2 + N // 2 * int(rng.integers(0, 2))) % N
            if m == p: m = (m + N // 2) % N
        v[m][:, j] = 2.0 ** -4 * (1 + rng.random((128, 4))) * s * on
        v[p][:, j] = (2.0 ** 5 if p % 2 else -2.0 ** 5) * (1 + rng.random((128, 4))) * s
    return draw(rng, v, q)
def setup_inputs_one(rng):
    v, q = striped(data(rng)), queries(rng)
    s = np.where(q[0, :, :4].astype(np.float32) < 0, -1.0, 1.0)
    q[:, :, 4:8] = (np.abs(q[:, :, 4:8].astype(np.float32)) * s).astype(BF)
    m, i = int(rng.integers(0, N)), np.arange(P)
    at = rng.permutation(np.flatnonzero((i % N != m) & ((i - m + 1) % N != m)))[:2 * K]
    size = np.repeat([2.0 ** 16, 2.0 ** 11], K)
    v[m][:, at] = (1 + rng.random((128, 2 * K, 4))) * s[:, None] * size[:, None]
    return draw(rng, v, q)
def setup_inputs_spread(rng):
    q = (queries(rng).astype(np.float32) * np.float32(2.0 ** 20)).astype(BF)
    return draw(rng, wide(rng, N, 128, 4 * P, cols=6), q)
def setup_inputs_ties(rng):
    v, q = np.zeros((N, 128, P, 4), np.float32), queries(rng)
    s = np.where(q[0, :, 4:8].astype(np.float32) < 0, -1.0, 1.0)
    q[:, :32, :4] = 0
    on = (np.arange(128) < 32)[:, None]
    for p in range(N):
        at = p + N * rng.permutation(P // N)
        for g in range(P // N // 3):
            x = 2.0 ** -2 * rng.standard_normal((N, 128, 1, 4))
            a, b, m = (p + 1 + rng.permutation(N - 1)[:3]) % N
            x[p] *= 2.0 ** 22
            x[m] = x[p]
            x[a, :, 0] = np.where(on, 2.0 ** 23 * (1 + rng.random((128, 4))) * s, x[a, :, 0])
            x[b] = x[a] * rng.choice([-1.0, 1.0])
            v[:, :, at[3 * g:3 * g + 3]] = x * rng.choice([-1.0, 1.0], (3, 1))
    return draw(rng, v, q)
def setup_inputs_zero(rng):
    v = striped(data(rng))
    lo, hi = int(rng.integers(0, K // 4 + 1)), int(rng.integers(K // 2, P - K // 4 + 1))
    v[:, :, :hi] = 0
    v[:, :, hi + K // 4:] = 0
    for j in range(lo, lo + K // 4):
        m, n = (j + 1 + rng.permutation(N - 1)[:2]) % N
        v[m][:, j] = 4 * rng.standard_normal((128, 4))
        v[n][:, j] = -v[m][:, j]
    harm(rng, v, np.arange(hi, hi + K // 4), 8)
    return draw(rng, v)
def check_inputs(d):
    b = []
    for k, lo, hi in (("tb", -16, 24), ("u", -30, 30), ("w", -30, 30)):
        v = np.abs(d[k].astype(np.float32))
        if not (np.isfinite(v).all() and ((v == 0) | (v >= 2.0 ** lo) & (v <= 2.0 ** hi)).all()): b.append("a value of " + k)
    q = d["u"].astype(np.float32)
    if (q[:, :, 8:] != 0).any(): b.append("u has numbers behind its first 2 columns")
    if (q != q[:1]).any(): b.append("u isn't the same on all ranks")
    return b
def reference(tb, u, w):
    tab = [mx_ref.quantize(np.ascontiguousarray(tb[r])) for r in range(N)]
    bs = np.zeros((N, 4, K), np.float32)
    for t in range(2):
        c, g = checks(tab, u)
        bad, lost = judge(c, g, t)
        new = rebuilt(tab, bad, lost, t)
        at = places(t, bad)
        for r in range(N):
            e = np.flatnonzero(lost == r)
            tab[r] = put(tab[r], at[r, e], pick(new, e))
        bs[:, 2 * t] = bad
        bs[:, 2 * t + 1] = lost
    oc, osc, y = np.zeros((N, 128, 4 * P), np.uint8), np.zeros((N, 16, P), np.uint8), np.zeros((N, 128, O * P), np.float32)
    for r in range(N):
        oc[r], osc[r] = emit(tab[r])
        for o in range(O):
            y[r, :, o * P:o * P + P] = mx_ref.matmul(mx_ref.quantize(np.ascontiguousarray(cut(w[r], o))), tab[r])
    return {"oc": oc, "osc": osc, "bs": bs, "y": y}

@@ -1,0 +1,560 @@
+import numpy as np
+from concourse.bass import DstId, RemoteDMATransfer
+from concourse.mybir import dt, AluOpType as Op, AxisListType, ActivationFunctionType as AF
+
+N, P, K = 8, 128, 32
+REB = ((0, 2, 4, 6), (1, 3, 5, 7))
+NK = K // 4
+X4, U8, F32, I32, U16, BF = "float8_e4m3fn_x4", "uint8", "float32", "int32", "uint16", "bfloat16"
+
+
+def _sb(n, d):
+    return ("sbuf", [128, n], d)
+
+
+SCRATCH = {
+    "tbt": _sb(544, BF), "ut": _sb(512, BF), "wt": _sb(512, BF), "hz": _sb(512, BF), "eb": _sb(2048, BF),
+    "t0": _sb(128, X4), "t0s": _sb(128, U8), "tr": _sb(128, X4), "trs": _sb(128, U8),
+    "uq": _sb(128, X4), "uqs": _sb(128, U8), "wq": _sb(128, X4), "wqs": _sb(128, U8),
+    "eq": _sb(512, X4), "eqs": _sb(512, U8),
+    "ur": _sb(256, X4), "urs": _sb(256, U8),
+    "t1": _sb(128, X4), "t1s": _sb(128, U8), "t2": _sb(128, X4), "t2s": _sb(128, U8),
+    "ones": _sb(304, F32), "ident": _sb(128, F32), "ck": _sb(64, F32),
+    "pi": _sb(2, I32), "pj": _sb(4, I32), "cf": _sb(8, F32), "mk": _sb(4, F32), "rr": _sb(8, F32), "irow": _sb(32, F32),
+    "pr": _sb(8, I32), "prb": _sb(8, I32), "xr": _sb(16, F32), "xi": _sb(16, I32), "xj": _sb(16, I32), "kw": _sb(256, F32), "pf": _sb(1, F32),
+    "km": _sb(2, F32), "sel": _sb(2, F32), "wr": _sb(8, F32), "w0": _sb(8, F32), "dm": _sb(8, F32), "pm": _sb(8, F32),
+    "c1": _sb(16, F32), "src": _sb(16, F32), "tgt": _sb(16, F32), "lc": _sb(4, F32), "fac": _sb(128, F32), "seg": _sb(256, F32),
+    "d0": _sb(64, F32), "oz": _sb(16, U16),
+    "ag": _sb(16, F32), "agn": _sb(32, F32), "so": _sb(12, F32), "xo": _sb(300, F32), "xs": _sb(300, F32), "msk": _sb(288, F32),
+    "rep": _sb(9, F32), "junk": _sb(32, F32), "hit": _sb(160, F32), "hiti": _sb(64, I32), "gv": _sb(40, F32), "w40": _sb(40, F32), "gt": _sb(96, F32),
+    "ysb": _sb(128, F32),
+    "ps": ("psum", [128, 1024], F32), "da": ("psum", [128, 1536], F32), "db": ("psum", [128, 1536], F32),
+}
+for _t in "01":
+    SCRATCH.update({
+        "sc" + _t: _sb(32, X4), "ss" + _t: _sb(32, U8), "la" + _t: _sb(192, X4), "ls" + _t: _sb(192, U8),
+        "or" + _t: _sb(128, X4), "os" + _t: _sb(128, U8), "h" + _t: _sb(512, BF), "nq" + _t: _sb(128, X4), "ns" + _t: _sb(128, U8),
+        "tw" + _t: _sb(256, X4), "tws" + _t: _sb(256, U8), "sb" + _t: _sb(256, F32),
+        "ex" + _t: _sb(64, F32), "ar" + _t: _sb(128, F32), "thr" + _t: _sb(128, F32), "g" + _t: _sb(130, F32), "yb" + _t: _sb(96, F32),
+        "sm" + _t: _sb(32, F32), "of" + _t: _sb(2, U16), "vr" + _t: _sb(192, F32), "vi" + _t: _sb(96, I32), "bsb" + _t: _sb(64, F32),
+        "rl" + _t: _sb(96, F32), "ol" + _t: _sb(4, U16), "ei" + _t: _sb(784, F32), "oi" + _t: _sb(8, U16),
+    })
+SEMAPHORES = ["v", "a", "sl", "s_ck", "s_la0", "s_la1", "s_nw0", "s_nw1"] + ["e%d" % _i for _i in range(120)]
+
+
+def rank_program(g, core, T, topo):
+    rank = T.rank_of(core)
+    if rank is None:
+        return
+    V, A, PE, SY = g.vector, g.scalar, g.tensor, g.sync
+    X = AxisListType.X
+    used, nv, na, nsl, fin = [0], [0], [0], [0], []
+
+    def ev(ins, n=1):
+        s = T.sem["e%d" % used[0]]
+        used[0] += 1
+        ins.then_inc(s, n)
+        return (s, n)
+
+    def wait(q, *evs):
+        for s, n in evs:
+            q.wait_ge(s, n)
+
+    def v(ins):
+        ins.then_inc(T.sem.v, 1)
+        nv[0] += 1
+
+    def vw():
+        V.wait_ge(T.sem.v, nv[0])
+
+    def a(ins):
+        ins.then_inc(T.sem.a, 1)
+        na[0] += 1
+
+    def aw():
+        A.wait_ge(T.sem.a, na[0])
+
+    def ts(out, i0, s1, op0, s2=None, op1=None):
+        if op1 is None:
+            return V.tensor_scalar(out, i0, s1, None, op0)
+        return V.tensor_scalar(out, i0, s1, s2, op0, op1)
+
+    def u8(view):
+        return view.bitcast(dt.uint8)
+
+    others = [r for r in range(N) if r != rank]
+
+    def dst(r):
+        rid, pid = topo.addr(T.cores[r], core)
+        return DstId(rid=int(rid), pnc=int(pid))
+
+    def to_all(view, sem):
+        es = topo.engines(core, T.cores[others[0]])
+        m = int(topo.mask(core, T.cores[others[0]]))
+        src, out = view
+        g.remote_dma_fused([RemoteDMATransfer(dst_ids=[dst(r) for r in others], dma_engine_mask=m, remote_sem=sem, srcs=[src], dsts=[out for r in others])], local_sem=T.sem.sl)
+        nsl[0] += len(es)
+
+    def to_rebuilders(pairs, sem):
+        tr = []
+        for i, (r, s, d) in enumerate(pairs):
+            es = topo.engines(core, T.cores[r])
+            w = len(es) // 4
+            m = 0
+            for e in es[w * i:w * i + w]:
+                m |= 1 << e
+            tr.append(RemoteDMATransfer(dst_ids=[dst(r)], dma_engine_mask=m, remote_sem=sem, srcs=[s], dsts=[d]))
+            nsl[0] += w
+        g.remote_dma_fused(tr, local_sem=T.sem.sl)
+
+    EW = len(topo.engines(core, T.cores[others[0]]))
+
+    e_tb = ev(SY.dma_start(T.tbt[:, 0:512], T.tb[:, 0:512]), 16)
+    e_u0 = ev(A.dma_start(T.ut[:, 0:4], T.u[:, 0:4]), 16)
+    e_u1 = ev(A.dma_start(T.ut[:, 4:16], T.u[:, 0:12]), 16)
+    e_tb2 = ev(SY.dma_start(T.tbt[:, 512:544], T.tb[:, 0:32]), 16)
+    e_w = ev(SY.dma_start(T.wt[:], T.w[:, 0:512]), 16)
+
+    def iota(out, pat, base, cm, f=True):
+        if f:
+            return ev(g.iota(out, pat, base, cm, allow_small_or_imprecise_dtypes=True))
+        return ev(g.iota(out, pat, base, cm))
+    i_pi = iota(T.pi[:, 0:2], [[1, 2]], 0, 1, False)
+    i_rr = iota(T.rr[:, 0:8], [[1, 8]], 0, 0)
+    i_ir = iota(T.irow[:, 0:32], [[1, 32]], 0, 0)
+    i_pr = iota(T.pr[:, 0:8], [[1, 8]], 0, 1, False)
+    i_x0 = iota(T.xr[:, 0:8], [[16, 8]], rank, 0)
+    i_x1 = iota(T.xr[:, 8:16], [[16, 8]], P - rank, 0)
+    i_pf = iota(T.pf[:, 0:1], [[0, 1]], 0, 1)
+
+    v(V.memset(T.ut[:, 16:512], 0.0))
+    e_hz = ev(V.memset(T.hz[:], 0.0))
+    e_ones = ev(V.memset(T.ones[:], 1.0))
+    wait(g, e_ones)
+    e_id = ev(g.affine_select(T.ident[:], T.ones[:, 0:128], [[-1, 128]], Op.is_equal, 0.0, 0, 1))
+    i_kw = iota(T.kw[:, 0:256], [[0, 8], [1, 32]], P, 0)
+    wait(V, i_pi)
+    v(ts(T.pj[:, 0:1], T.pi[:, 0:1], 15, Op.bitwise_and))
+    v(ts(T.pj[:, 1:2], T.pi[:, 0:1], 31, Op.bitwise_and))
+    v(ts(T.pj[:, 2:3], T.pi[:, 0:1], 7, Op.bitwise_and))
+    v(ts(T.pj[:, 3:4], T.pi[:, 1:2], 7, Op.bitwise_and))
+    vw()
+    v(V.tensor_copy(T.cf[:, 0:4], T.pj[:, 0:4]))
+    vw()
+    p16, p32, p8, q1 = (T.cf[:, i:i + 1] for i in range(4))
+    v(ts(T.mk[:, 0:1], p8, float(rank), Op.is_equal))
+    v(ts(T.mk[:, 1:2], p8, float(rank), Op.not_equal))
+    v(ts(T.mk[:, 2:3], p8, float(rank), Op.not_equal))
+    v(V.memset(T.so[:, 8:12], 2.0 ** -120))
+    v(V.memset(T.xo[:, 297:300], 2.0 ** -120))
+    vw()
+    wait(V, e_u0, e_u1)
+    e_uq = ev(V.quantize_mx(T.uq[:], T.uqs[:], T.ut[:]))
+    wait(V, e_tb)
+    e_t0 = ev(V.quantize_mx(T.t0[:], T.t0s[:], T.tbt[:, 0:512]))
+    wait(V, e_tb2)
+    e_tr = ev(V.quantize_mx(T.tr[:], T.trs[:], T.tbt[:, 4 * rank:4 * rank + 512]))
+    wait(PE, e_uq, e_t0)
+    e_m0 = ev(PE.matmul_mx(T.ps[:, 0:128], T.t0[:], T.t0s[:], T.uq[:], T.uqs[:], True, True))
+    wait(PE, e_tr)
+    e_m1 = ev(PE.matmul_mx(T.ps[:, 512:640], T.tr[:], T.trs[:], T.uq[:], T.uqs[:], True, True))
+    o = 8 * rank
+    wait(V, e_m0)
+    e_c0 = ev(V.tensor_tensor(T.ck[:, o:o + 3], T.ps[:, 0:3], T.mk[:, 0:3], Op.mult))
+    wait(V, e_m1)
+    e_c1 = ev(V.tensor_copy(T.ck[:, o + 3:o + 5], T.ps[:, 513:515]))
+    wait(g, e_c0, e_c1)
+    to_all((T.ck[:, o:o + 5], T.ck[:, o:o + 5]), T.sem.s_ck)
+
+    wait(A, e_hz)
+    for b in range(4):
+        a(A.activation(T.eb[:, 512 * b:512 * b + 512], T.hz[:], AF.Copy))
+    wait(A, e_id)
+    aw()
+    for b in range(4):
+        a(A.activation(T.eb[:, 512 * b + b:512 * b + 512:4], T.ident[:], AF.Copy))
+    e_eb = ev(A.activation(T.h0[:], T.hz[:], AF.Copy))
+    e_eb2 = ev(A.activation(T.h1[:], T.hz[:], AF.Copy))
+
+    wait(V, e_hz, e_ones, e_uq, e_t0, e_tr, e_c0, e_c1)
+    mine = [t for t in range(2) if rank in REB[t]][0]
+    wait(V, i_rr, i_ir, i_pr, i_x0, i_x1, i_pf, i_kw)
+    v(ts(T.wr[:], T.rr[:], -1.0 / 8192, Op.mult, 8.0 / 8192, Op.add))
+    v(ts(T.gt[:, 0:8], T.rr[:], p8, Op.not_equal))
+    v(ts(T.dm[:], T.rr[:], q1, Op.not_equal))
+    v(ts(T.pm[:], T.rr[:], q1, Op.is_equal))
+    v(ts(T.fac[:, 0:32], T.irow[:], p32, Op.is_lt, -2.0 ** -24, Op.mult))
+    v(V.memset(T.fac[:, 32:128], 1.0))
+    v(ts(T.km[:, 0:1], p16, 0.0, Op.add))
+    v(ts(T.km[:, 1:2], p16, 16.0, Op.add))
+    v(ts(T.sel[:, 0:1], p32, 16.0, Op.is_lt))
+    v(ts(T.sel[:, 1:2], p32, 16.0, Op.is_ge))
+    v(ts(T.g0[:, 128:129], T.pf[:], 1.0 / 256, Op.mult))
+    v(ts(T.g1[:, 128:129], T.pf[:], 1.0 / 256, Op.mult))
+    vw()
+    v(V.tensor_tensor(T.w0[:], T.gt[:, 0:8], T.wr[:], Op.mult))
+    v(ts(T.fac[:, 0:32], T.fac[:, 0:32], 1.0, Op.add))
+    for b in range(1, 4):
+        v(V.memset(T.fac[32 * b:32 * b + 32, 128 - 32 * b:128], 1.0 - 2.0 ** -24))
+    e_fac = ev(V.memset(T.oz[:, 0:8], 0))
+    v(V.memset(T.oz[:, 8:16], 2))
+    vw()
+    wait(V, e_fac)
+    v(V.quantize_mx(T["tw0"][:, 0:128], T["tws0"][:, 0:128], T.tbt[:, 0:512]))
+    v(V.quantize_mx(T["tw0"][:, 128:256], T["tws0"][:, 128:256], T.hz[:]))
+    v(V.quantize_mx(T["la%d" % mine][:, 64:192], T["ls%d" % mine][:, 64:192], T.hz[:]))
+    v(V.quantize_mx(T["or%d" % mine][:], T["os%d" % mine][:], T.hz[:]))
+    v(V.memset(T.d0[:], 1.0))
+    v(V.memset(T.seg[:], 1.0))
+    v(ts(T.lc[:, 0:1], p8, -1.0, Op.add))
+    v(ts(T.lc[:, 1:2], p8, 0.0, Op.is_equal))
+    v(ts(T.lc[:, 2:3], p16, 8.0, Op.is_lt))
+    v(ts(T.lc[:, 3:4], p16, 8.0, Op.is_ge))
+    vw()
+    v(V.memset(T.d0[:, 0:64:8], 0.0))
+    v(V.memset(T.d0[:, 1:64:8], -1.0))
+    v(V.memset(T.seg[:, 0:256:32], 0.0))
+    wait(V, e_eb, e_eb2)
+    e_eq = ev(V.quantize_mx(T.eq[:], T.eqs[:], T.eb[:]))
+    vw()
+    im1, is0, lo8, hi8 = (T.lc[:, i:i + 1] for i in range(4))
+
+    def late_constants():
+        v(ts(T.prb[:], T.pr[:], 127, Op.bitwise_and))
+        v(ts(T.xi[:], T.xr[:], p16, Op.add))
+        vw()
+        v(V.tensor_copy(T.c1[:, 0:8], T.prb[:]))
+        v(ts(T.xj[:], T.xi[:], 127, Op.bitwise_and))
+        vw()
+        v(ts(T.c1[:, 8:16], T.c1[:, 0:8], 1.0 / 256, Op.mult))
+        v(V.tensor_copy(T.src[:], T.xj[:]))
+        vw()
+        v(V.tensor_tensor(T.c1[:, 0:8], T.c1[:, 8:16], T.wr[:], Op.add))
+        v(ts(T.tgt[:], T.src[:], 1.0 / 256, Op.mult, (8 - rank) / 8192.0, Op.add))
+        vw()
+        v(V.tensor_tensor(T.c1[:, 8:16], T.c1[:, 0:8], T.pm[:], Op.mult))
+        vw()
+        v(V.tensor_reduce(T.cf[:, 4:5], T.c1[:, 8:16], X, Op.add))
+        e = ev(V.tensor_copy(T.ur[:, 0:128].bitcast(dt.uint32), T.uq[:, 0:128].bitcast(dt.uint32).indirect(T.oz[:, 0:8])))
+        e2 = ev(V.tensor_copy(T.ur[:, 128:256].bitcast(dt.uint32), T.uq[:, 0:128].bitcast(dt.uint32).indirect(T.oz[:, 8:16])))
+        v(V.quantize_mx(T.wq[:], T.wqs[:], T.wt[:]))
+        vw()
+        return e, e2
+
+    wait(A, e_uq, e_fac)
+    wait(V, e_w)
+    e_ur = late_constants()
+    wait(A, *e_ur)
+    e_us0 = ev(A.activation(T.urs[:, 0:128], T.uqs[:, 0:128].indirect(T.oz[:, 0:8]), AF.Copy))
+    e_us1 = ev(A.activation(T.urs[:, 128:256], T.uqs[:, 0:128].indirect(T.oz[:, 8:16]), AF.Copy))
+
+    def rotate(buf, w):
+        for n in range(4):
+            m = (n + 1) % 4
+            v(V.tensor_copy(buf[32 * n:32 * n + 32, w:2 * w], buf[32 * m:32 * m + 32, 0:w]))
+        vw()
+        v(V.tensor_copy(buf[0:64, 2 * w:4 * w], buf[64:128, 0:2 * w]))
+        v(V.tensor_copy(buf[64:128, 2 * w:4 * w], buf[0:64, 0:2 * w]))
+        vw()
+
+    def order(t, s2, lost):
+        ex, ar, thr, gg, yb, sm = (T["%s%d" % (n, t)] for n in ("ex", "ar", "thr", "g", "yb", "sm"))
+        e_a = ev(V.tensor_reduce(sm[:, 0:1], s2, X, Op.max, apply_absolute_value=True))
+        wait(A, e_a, e_fac)
+        e_th = ev(A.activation(thr[:], T.fac[:], AF.Copy, scale=sm[:, 0:1]))
+        wait(V, e_a)
+        v(ts(ex[:, 0:32], T.ones[:, 0:32], sm[:, 0:1], Op.mult))
+        vw()
+        v(V.transpose(ar[:, 0:32], ex[:, 0:32]))
+        vw()
+        rotate(ar, 32)
+        lost()
+        wait(V, e_th)
+        v(V.tensor_tensor(gg[:, 0:128], ar[:], thr[:], Op.is_gt))
+        vw()
+        v(V.tensor_reduce(sm[:, 1:2], gg[:, 0:130], X, Op.add))
+        vw()
+        v(ts(ex[:, 32:64], T.ones[:, 0:32], sm[:, 1:2], Op.mult))
+        vw()
+        v(V.transpose(yb[:, 0:32], ex[:, 32:64]))
+        vw()
+        v(ts(yb[:, 32:64], yb[:, 0:32], T.km[:, 0:1], Op.subtract))
+        v(ts(yb[:, 64:96], yb[:, 0:32], T.km[:, 1:2], Op.subtract))
+        vw()
+        z = sm[:, 8:16]
+        v(V.tensor_reduce(sm[:, 8:9], yb[:, 32:64], X, Op.min, apply_absolute_value=True))
+        v(V.tensor_reduce(sm[:, 9:10], yb[:, 64:96], X, Op.min, apply_absolute_value=True))
+        vw()
+        for n in range(4):
+            m = (n + 1) % 4
+            v(V.tensor_copy(sm[32 * n:32 * n + 32, 10:12], sm[32 * m:32 * m + 32, 8:10]))
+        vw()
+        v(V.tensor_copy(sm[0:64, 12:16], sm[64:128, 8:12]))
+        v(V.tensor_copy(sm[64:128, 12:16], sm[0:64, 8:12]))
+        vw()
+        v(V.tensor_reduce(sm[:, 16:17], sm[:, 8:16:2], X, Op.min))
+        v(V.tensor_reduce(sm[:, 17:18], sm[:, 9:16:2], X, Op.min))
+        vw()
+        of = T["of%d" % t]
+        e_of = ev(ts(of[:], sm[:, 16:18], 256.0, Op.mult))
+        wait(V, e_of)
+        wait(A, e_of)
+        tab, tabs, e_tab = (T.t0, T.t0s, [e_t0]) if t == 0 else (T.t1, T.t1s, e_t1)
+        sc, ss, la, ls = (T["%s%d" % (n, t)] for n in ("sc", "ss", "la", "ls"))
+        wait(V, *e_tab)
+        wait(A, *e_tab)
+        e_sc = ev(V.tensor_copy(sc[:].bitcast(dt.uint32), tab[:, 0:128].bitcast(dt.uint32).indirect(of[:])))
+        e_ss = ev(A.activation(ss[:], tabs[:, 0:128].indirect(of[:]), AF.Copy))
+        sl = slice(NK * rank, NK * rank + NK)
+        wait(g, e_sc)
+        to_rebuilders([(r, u8(sc[:, NK * i:NK * i + NK]), u8(la[:, sl])) for i, r in enumerate(REB[t]) if r != rank], T.sem["s_la%d" % t])
+        wait(g, e_ss)
+        to_rebuilders([(r, ss[:, NK * i:NK * i + NK], ls[:, sl]) for i, r in enumerate(REB[t]) if r != rank], T.sem["s_la%d" % t])
+        own = []
+        if rank in REB[t]:
+            i = REB[t].index(rank)
+            wait(SY, e_sc)
+            own.append(ev(SY.dma_start(u8(la[:, sl]), u8(sc[:, NK * i:NK * i + NK])), 16))
+            wait(SY, e_ss)
+            own.append(ev(SY.dma_start(ls[:, sl], ss[:, NK * i:NK * i + NK]), 16))
+        vr, vi, bsb = T["vr%d" % t], T["vi%d" % t], T["bsb%d" % t]
+        v(V.tensor_tensor(sm[:, 20:22], sm[:, 16:18], T.sel[:], Op.mult))
+        vw()
+        v(V.tensor_reduce(sm[:, 22:23], sm[:, 20:22], X, Op.add))
+        vw()
+        v(ts(vr[:, 0:32], T.ones[:, 0:32], sm[:, 22:23], Op.mult))
+        vw()
+        v(V.transpose(vr[:, 32:64], vr[:, 0:32]))
+        vw()
+        v(ts(vr[:, 64:96], vr[:, 32:64], 256.0, Op.mult))
+        vw()
+        v(V.tensor_copy(vi[:, 0:32], vr[:, 64:96]))
+        vw()
+        v(V.tensor_copy(bsb[:, 0:32], vi[:, 0:32]))
+        v(ts(vi[:, 32:64], vi[:, 0:32], t, Op.add))
+        vw()
+        v(V.tensor_tensor(vr[:, 96:128], vr[:, 64:96], bsb[:, 0:32], Op.subtract))
+        v(ts(vi[:, 64:96], vi[:, 32:64], 7, Op.bitwise_and))
+        vw()
+        e_b = ev(ts(bsb[:, 32:64], vr[:, 96:128], -32.0, Op.mult, 8.0, Op.add))
+        v(V.tensor_copy(vr[:, 128:160], vi[:, 64:96]))
+        vw()
+        wait(V, e_b)
+        wait(SY, e_b)
+        fin.append(ev(SY.dma_start(T.bs[2 * t:2 * t + 2, 0:32], bsb[0:1, 0:64]), 16))
+        return own
+
+    def rebuild_list(t):
+        s = NK * REB[t].index(rank)
+        vr, bsb, rl, ol = T["vr%d" % t], T["bsb%d" % t], T["rl%d" % t], T["ol%d" % t]
+        q, lost = vr[:, 128 + s:136 + s], bsb[:, 32 + s:40 + s]
+        v(ts(rl[:, 0:8], q, im1, Op.is_le, im1, Op.add))
+        v(ts(rl[:, 8:16], q, is0, Op.mult))
+        vw()
+        v(V.tensor_tensor(rl[:, 16:24], rl[:, 0:8], rl[:, 8:16], Op.max))
+        vw()
+        v(V.tensor_tensor(rl[:, 24:32], rl[:, 16:24], lost, Op.is_equal))
+        v(ts(rl[:, 32:40], rl[:, 16:24], float(NK), Op.mult))
+        vw()
+        v(ts(rl[:, 40:48], rl[:, 24:32], 64.0, Op.mult))
+        v(V.tensor_tensor(rl[:, 48:56], rl[:, 32:40], T.rr[:], Op.add))
+        vw()
+        v(V.tensor_tensor(rl[:, 56:64], rl[:, 40:48], rl[:, 48:56], Op.max))
+        vw()
+        v(ts(rl[:, 64:68], rl[:, 56:64:2], lo8, Op.mult))
+        v(ts(rl[:, 68:72], rl[:, 57:64:2], hi8, Op.mult))
+        vw()
+        v(V.tensor_tensor(rl[:, 72:76], rl[:, 64:68], rl[:, 68:72], Op.add))
+        vw()
+        e = ev(V.tensor_copy(ol[:], rl[:, 72:76]))
+        wait(V, e)
+        return e
+
+    def rebuild(t, own, e_ol):
+        la, ls, od, os_, h, nq, ns, sb, ol = (T["%s%d" % (n, t)] for n in ("la", "ls", "or", "os", "h", "nq", "ns", "sb", "ol"))
+        D = T.da if t == 0 else T.db
+        arr = (T.sem["s_la%d" % t], 7 * 2 * (EW // 4))
+        wait(V, arr, *own)
+        e_oc = ev(V.tensor_copy(od[:, 0:64].bitcast(dt.uint32), la[:, 0:96].bitcast(dt.uint32).indirect(ol[:])))
+        wait(A, e_ol, arr, *own)
+        e_os = ev(A.activation(os_[:, 0:64], ls[:, 0:96].indirect(ol[:]), AF.Copy))
+        wait(PE, e_eq, e_oc, e_os)
+        scans = []
+        for b in range(4):
+            k = 512 * (b % 3)
+            if b == 3:
+                wait(PE, scans[0])
+            e_d = ev(PE.matmul_mx(D[:, k:k + 128], T.eq[:, 128 * b:128 * b + 128], T.eqs[:, 128 * b:128 * b + 128], od[:], os_[:], True, True))
+            wait(V, e_d)
+            e = ev(V.tensor_tensor_scan(sb[:, 64 * b:64 * b + 64], T.d0[:], D[:, k:k + 64], 0.0, Op.mult, Op.subtract))
+            scans.append(e)
+            wait(V, e)
+            v(V.tensor_copy(h[:, b:4 * NK:4], sb[:, 64 * b + 7:64 * b + 64:8]))
+        vw()
+        e_nq = ev(V.quantize_mx(nq[:], ns[:], h[:]))
+        wait(V, e_nq)
+        i = REB[t].index(rank)
+        sl = slice(P + NK * i, P + NK * i + NK)
+        tw, tws = T["tw%d" % t], T["tws%d" % t]
+        wait(g, e_nq)
+        to_all((u8(nq[:, 0:NK]), u8(tw[:, sl])), T.sem["s_nw%d" % t])
+        to_all((ns[:, 0:NK], tws[:, sl]), T.sem["s_nw%d" % t])
+        wait(SY, e_nq)
+        return [ev(SY.dma_start(u8(tw[:, sl]), u8(nq[:, 0:NK])), 16), ev(SY.dma_start(tws[:, sl], ns[:, 0:NK]), 16)]
+
+    def table_list(t):
+        vr, ei, oi = T["vr%d" % t], T["ei%d" % t], T["oi%d" % t]
+        for c in range(8):
+            v(ts(ei[:, 32 * c:32 * c + 32], vr[:, 32:64], T.tgt[:, 8 * t + c:8 * t + c + 1], Op.is_equal))
+        vw()
+        v(V.tensor_tensor(ei[:, 256:512], ei[:, 0:256], T.kw[:], Op.mult))
+        vw()
+        v(V.tensor_tensor_scan(ei[:, 512:768], T.seg[:], ei[:, 256:512], 0.0, Op.mult, Op.max))
+        vw()
+        v(V.tensor_tensor(ei[:, 768:776], ei[:, 543:768:32], T.src[:, 8 * t:8 * t + 8], Op.max))
+        vw()
+        e = ev(V.tensor_copy(oi[:], ei[:, 768:776]))
+        wait(V, e)
+        return e
+
+    s_ck = (T.sem.s_ck, 7 * EW)
+    wait(A, s_ck, e_c0, e_c1)
+    e_ag0 = ev(A.activation(T.ag[:, 0:8], T.ck[:, 2:64:8], AF.Abs))
+    e_ag1 = ev(A.activation(T.ag[:, 8:16], T.ck[:, 4:64:8], AF.Abs))
+    wait(V, s_ck)
+    v(V.tensor_reduce(T.cf[:, 5:6], T.ck[:, 0:64:8], X, Op.add))
+    vw()
+    v(V.tensor_tensor_scan(T.so[:, 0:8], T.ones[:, 0:8], T.ck[:, 1:64:8], T.cf[:, 5:6], Op.mult, Op.subtract))
+    vw()
+
+    def lost0():
+        wait(V, e_ag0)
+        v(V.tensor_reduce(T.cf[:, 6:7], T.ag[:, 0:8], X, Op.max))
+        vw()
+        v(ts(T.gt[:, 8:16], T.ag[:, 0:8], T.cf[:, 6:7], Op.is_equal))
+        vw()
+        v(V.tensor_tensor(T.gt[:, 16:24], T.gt[:, 8:16], T.w0[:], Op.mult))
+        vw()
+        v(V.tensor_reduce(T.g0[:, 129:130], T.gt[:, 16:24], X, Op.max))
+        vw()
+
+    own = order(0, T.so[:, 7:9], lost0)
+    if mine == 0:
+        e_ol = rebuild_list(0)
+    codeq = T.cf[:, 4:5]
+    vr = T["vr0"]
+    e_ms = []
+    for r in range(N):
+        e_ms.append(ev(ts(T.msk[:, 32 * r:32 * r + 32], vr[:, 32:64], T.c1[:, r:r + 1], Op.is_equal, T.dm[:, r:r + 1], Op.mult)))
+    e_ms.append(ev(ts(T.msk[:, 256:288], vr[:, 32:64], codeq, Op.is_equal, -1.0, Op.mult)))
+    new_own = []
+    if mine == 0:
+        wait(V, *e_ms)
+        new_own = rebuild(0, own, e_ol)
+    else:
+        wait(V, *e_ms)
+    for r in range(N + 1):
+        wait(A, e_ms[r])
+        if r:
+            aw()
+        a(A.activation(T.junk[:], T.msk[:, 32 * r:32 * r + 32], AF.Copy, accum_out=T.rep[:, r:r + 1]))
+    aw()
+    e_rep = ev(A.activation(T.gt[:, 64:72], T.rep[:, 0:8], AF.Copy))
+    hit, hi = T.hit, T.hiti
+    bsb = T["bsb0"]
+    v(V.tensor_tensor(hit[:, 0:32], bsb[:, 0:32], bsb[:, 32:64], Op.subtract))
+    v(ts(hit[:, 32:64], bsb[:, 32:64], q1, Op.not_equal))
+    v(V.tensor_tensor(T.gt[:, 24:32], T.ck[:, 3:64:8], T.pm[:], Op.mult))
+    vw()
+    v(ts(hi[:, 0:32], hit[:, 0:32], 128.0, Op.add))
+    v(V.tensor_reduce(T.cf[:, 7:8], T.gt[:, 24:32], X, Op.add))
+    vw()
+    v(ts(hi[:, 32:64], hi[:, 0:32], 127, Op.bitwise_and))
+    wait(V, e_rep)
+    v(V.tensor_tensor(T.gt[:, 32:40], T.dm[:], T.gt[:, 64:72], Op.subtract))
+    v(ts(T.gt[:, 40:41], T.rep[:, 8:9], 1.0, Op.add, -1.0, Op.mult))
+    vw()
+    v(V.tensor_copy(hit[:, 64:96], hi[:, 32:64]))
+    v(V.tensor_tensor(T.xs[:, 65:297:33], T.ck[:, 3:64:8], T.gt[:, 32:40], Op.mult))
+    v(V.tensor_tensor(T.w40[:, 0:8], T.gt[:, 32:40], T.wr[:], Op.mult))
+    wait(V, e_ag1)
+    v(V.tensor_tensor(T.gv[:, 0:8], T.gt[:, 32:40], T.ag[:, 8:16], Op.mult))
+    v(V.tensor_tensor(T.xs[:, 32:33], T.cf[:, 7:8], T.gt[:, 40:41], Op.mult))
+    vw()
+    v(ts(hit[:, 96:128], hit[:, 64:96], T.pf[:, 0:1], Op.is_equal))
+    vw()
+    v(V.tensor_tensor(hit[:, 128:160], hit[:, 96:128], hit[:, 32:64], Op.mult))
+    vw()
+    v(V.tensor_tensor(hit[:, 0:32], hit[:, 128:160], vr[:, 96:128], Op.mult))
+    vw()
+    v(ts(T.w40[:, 8:40], hit[:, 0:32], 1.0 / 256, Op.mult))
+    vw()
+    e_oi = table_list(0)
+
+    def arrived(t):
+        return (T.sem["s_nw%d" % t], 2 * EW * (4 - (1 if mine == t else 0)))
+    nw = arrived(0)
+    wait(PE, nw, *new_own)
+    wait(PE, e_us0, e_us1, *e_ur)
+    wait(PE, e_c0, e_c1)
+    e_cn = ev(PE.matmul_mx(T.ps[:, 0:128], T.ur[:, 0:128], T.urs[:, 0:128], T["tw0"][:, 128:256], T["tws0"][:, 128:256], True, True))
+    e_gn = ev(PE.matmul_mx(T.ps[:, 512:640], T.ur[:, 128:256], T.urs[:, 128:256], T["tw0"][:, 128:256], T["tws0"][:, 128:256], True, True))
+    wait(V, nw, *new_own)
+    p1 = ev(V.tensor_copy(T.t1[:].bitcast(dt.uint32), T["tw0"][:, 0:160].bitcast(dt.uint32).indirect(T.oi0[:])))
+    wait(A, nw, e_oi, *new_own)
+    p2 = ev(A.activation(T.t1s[:], T["tws0"][:, 0:160].indirect(T.oi0[:]), AF.Copy))
+    e_t1 = [p1, p2]
+    wait(A, e_gn)
+    e_agn = ev(A.activation(T.agn[:], T.ps[:, 512:544], AF.Abs))
+    wait(SY, p1, p2)
+    e_tw = [ev(SY.dma_start(u8(T["tw1"][:, 0:128]), u8(T.t1[:])), 16), ev(SY.dma_start(T["tws1"][:, 0:128], T.t1s[:]), 16)]
+    wait(V, e_cn)
+    v(V.tensor_tensor(T.xs[:, 0:32], T.msk[:, 256:288], T.ps[:, 0:32], Op.mult))
+    for r in range(N - 1):
+        v(V.tensor_tensor(T.xs[:, 33 + 33 * r:65 + 33 * r], T.msk[:, 32 * r:32 * r + 32], T.ps[:, 0:32], Op.mult))
+    r = N - 1
+    e_xp = ev(V.tensor_tensor(T.xs[:, 33 + 33 * r:65 + 33 * r], T.msk[:, 32 * r:32 * r + 32], T.ps[:, 0:32], Op.mult))
+    vw()
+    wait(V, e_xp)
+    v(V.tensor_tensor_scan(T.xo[:, 0:297], T.ones[:, 0:297], T.xs[:, 0:297], 0.0, Op.mult, Op.subtract))
+    vw()
+
+    def lost1():
+        wait(V, e_agn)
+        v(V.tensor_tensor(T.gv[:, 8:40], T.agn[:], hit[:, 128:160], Op.mult))
+        vw()
+        v(V.tensor_reduce(T.gt[:, 42:43], T.gv[:], X, Op.max))
+        vw()
+        v(ts(T.ex0[:, 0:40], T.gv[:], T.gt[:, 42:43], Op.is_equal))
+        vw()
+        v(V.tensor_tensor(T.yb0[:, 0:40], T.ex0[:, 0:40], T.w40[:], Op.mult))
+        vw()
+        v(V.tensor_reduce(T.g1[:, 129:130], T.yb0[:, 0:40], X, Op.max))
+        vw()
+
+    own = order(1, T.xo[:, 296:298], lost1)
+    new_own = []
+    if mine == 1:
+        e_ol = rebuild_list(1)
+        new_own = rebuild(1, own, e_ol)
+    e_oi = table_list(1)
+    nw = arrived(1)
+    wait(V, nw, *new_own)
+    wait(V, *e_tw)
+    p1 = ev(V.tensor_copy(T.t2[:].bitcast(dt.uint32), T["tw1"][:, 0:160].bitcast(dt.uint32).indirect(T.oi1[:])))
+    wait(A, nw, e_oi, *new_own)
+    wait(A, *e_tw)
+    p2 = ev(A.activation(T.t2s[:], T["tws1"][:, 0:160].indirect(T.oi1[:]), AF.Copy))
+    wait(SY, p1)
+    fin.append(ev(SY.dma_start(T.oc[:, 0:512], u8(T.t2[:])), 16))
+    wait(A, p2)
+    for k in range(4):
+        fin.append(ev(A.dma_start(T.osc[4 * k:4 * k + 4, 0:128], T.t2s[32 * k:32 * k + 4, 0:128]), 16))
+    wait(PE, p1, p2, e_xp)
+    e_y = ev(PE.matmul_mx(T.ps[:, 0:128], T.wq[:], T.wqs[:], T.t2[:], T.t2s[:], True, True))
+    wait(V, e_y)
+    e_yc = ev(V.tensor_copy(T.ysb[:], T.ps[:, 0:128]))
+    wait(SY, e_yc)
+    fin.append(ev(SY.dma_start(T.y[:, 0:128], T.ysb[:]), 16))
+    wait(g, *fin)
+    g.wait_ge(T.sem.sl, nsl[0])

@@ -5,6 +5,7 @@ from concourse.mybir import dt, AluOpType as Op, AxisListType, ActivationFunctio
 N, P, K = 8, 128, 32
 REB = ((0, 2, 4, 6), (1, 3, 5, 7))
 NK = K // 4
+TINY = 2.0 ** -121
 X4, U8, F32, I32, U16, BF = "float8_e4m3fn_x4", "uint8", "float32", "int32", "uint16", "bfloat16"
 
 
@@ -22,12 +23,12 @@ SCRATCH = {
     "ones": _sb(304, F32), "ident": _sb(128, F32), "ck": _sb(64, F32),
     "pi": _sb(2, I32), "pj": _sb(4, I32), "cf": _sb(8, F32), "mk": _sb(4, F32), "rr": _sb(8, F32), "irow": _sb(32, F32),
     "pr": _sb(8, I32), "prb": _sb(8, I32), "xr": _sb(16, F32), "xi": _sb(16, I32), "xj": _sb(16, I32), "kw": _sb(256, F32), "pf": _sb(1, F32),
-    "km": _sb(2, F32), "sel": _sb(2, F32), "wr": _sb(8, F32), "w0": _sb(8, F32), "dm": _sb(8, F32), "pm": _sb(8, F32),
+    "sel": _sb(2, F32), "wr": _sb(8, F32), "w0": _sb(8, F32), "dm": _sb(8, F32), "pm": _sb(8, F32),
     "c1": _sb(16, F32), "src": _sb(16, F32), "tgt": _sb(16, F32), "lc": _sb(4, F32), "fac": _sb(128, F32), "seg": _sb(256, F32),
     "d0": _sb(64, F32), "oz": _sb(16, U16),
     "ag": _sb(16, F32), "agn": _sb(32, F32), "so": _sb(12, F32), "xo": _sb(300, F32), "xs": _sb(300, F32), "msk": _sb(288, F32),
     "rep": _sb(9, F32), "junk": _sb(32, F32), "hit": _sb(160, F32), "hiti": _sb(64, I32), "gv": _sb(40, F32), "w40": _sb(40, F32), "gt": _sb(96, F32),
-    "ysb": _sb(128, F32),
+    "lw": _sb(96, F32), "ysb": _sb(128, F32),
     "ps": ("psum", [128, 1024], F32), "da": ("psum", [128, 1536], F32), "db": ("psum", [128, 1536], F32),
 }
 for _t in "01":
@@ -35,11 +36,11 @@ for _t in "01":
         "sc" + _t: _sb(32, X4), "ss" + _t: _sb(32, U8), "la" + _t: _sb(192, X4), "ls" + _t: _sb(192, U8),
         "or" + _t: _sb(128, X4), "os" + _t: _sb(128, U8), "h" + _t: _sb(512, BF), "nq" + _t: _sb(128, X4), "ns" + _t: _sb(128, U8),
         "tw" + _t: _sb(256, X4), "tws" + _t: _sb(256, U8), "sb" + _t: _sb(256, F32),
-        "ex" + _t: _sb(64, F32), "ar" + _t: _sb(128, F32), "thr" + _t: _sb(128, F32), "g" + _t: _sb(130, F32), "yb" + _t: _sb(96, F32),
-        "sm" + _t: _sb(32, F32), "of" + _t: _sb(2, U16), "vr" + _t: _sb(192, F32), "vi" + _t: _sb(96, I32), "bsb" + _t: _sb(64, F32),
-        "rl" + _t: _sb(96, F32), "ol" + _t: _sb(4, U16), "ei" + _t: _sb(784, F32), "oi" + _t: _sb(8, U16),
+        "ex" + _t: _sb(32, F32), "ar" + _t: _sb(128, F32), "thr" + _t: _sb(128, F32), "g" + _t: _sb(193, F32), "yo" + _t: _sb(193, F32),
+        "yb" + _t: _sb(64, F32), "sm" + _t: _sb(32, F32), "of" + _t: _sb(2, U16), "vr" + _t: _sb(192, F32), "vi" + _t: _sb(96, I32),
+        "bsb" + _t: _sb(64, F32), "rl" + _t: _sb(96, F32), "ol" + _t: _sb(4, U16), "ei" + _t: _sb(784, F32), "oi" + _t: _sb(8, U16),
     })
-SEMAPHORES = ["v", "a", "sl", "s_ck", "s_la0", "s_la1", "s_nw0", "s_nw1"] + ["e%d" % _i for _i in range(120)]
+SEMAPHORES = ["v", "a", "sl", "s_ck", "s_la0", "s_la1", "s_nw0", "s_nw1"] + ["e%d" % _i for _i in range(130)]
 
 
 def rank_program(g, core, T, topo):
@@ -82,18 +83,20 @@ def rank_program(g, core, T, topo):
     def u8(view):
         return view.bitcast(dt.uint8)
 
+    def u32(view):
+        return view.bitcast(dt.uint32)
+
     others = [r for r in range(N) if r != rank]
+    EW = len(topo.engines(core, T.cores[others[0]]))
 
     def dst(r):
         rid, pid = topo.addr(T.cores[r], core)
         return DstId(rid=int(rid), pnc=int(pid))
 
-    def to_all(view, sem):
-        es = topo.engines(core, T.cores[others[0]])
+    def to_all(src, out, sem):
         m = int(topo.mask(core, T.cores[others[0]]))
-        src, out = view
         g.remote_dma_fused([RemoteDMATransfer(dst_ids=[dst(r) for r in others], dma_engine_mask=m, remote_sem=sem, srcs=[src], dsts=[out for r in others])], local_sem=T.sem.sl)
-        nsl[0] += len(es)
+        nsl[0] += EW
 
     def to_rebuilders(pairs, sem):
         tr = []
@@ -107,7 +110,7 @@ def rank_program(g, core, T, topo):
             nsl[0] += w
         g.remote_dma_fused(tr, local_sem=T.sem.sl)
 
-    EW = len(topo.engines(core, T.cores[others[0]]))
+    mine = [t for t in range(2) if rank in REB[t]][0]
 
     e_tb = ev(SY.dma_start(T.tbt[:, 0:512], T.tb[:, 0:512]), 16)
     e_u0 = ev(A.dma_start(T.ut[:, 0:4], T.u[:, 0:4]), 16)
@@ -122,10 +125,10 @@ def rank_program(g, core, T, topo):
     i_pi = iota(T.pi[:, 0:2], [[1, 2]], 0, 1, False)
     i_rr = iota(T.rr[:, 0:8], [[1, 8]], 0, 0)
     i_ir = iota(T.irow[:, 0:32], [[1, 32]], 0, 0)
+    i_pf = iota(T.pf[:, 0:1], [[0, 1]], 0, 1)
     i_pr = iota(T.pr[:, 0:8], [[1, 8]], 0, 1, False)
     i_x0 = iota(T.xr[:, 0:8], [[16, 8]], rank, 0)
     i_x1 = iota(T.xr[:, 8:16], [[16, 8]], P - rank, 0)
-    i_pf = iota(T.pf[:, 0:1], [[0, 1]], 0, 1)
 
     v(V.memset(T.ut[:, 16:512], 0.0))
     e_hz = ev(V.memset(T.hz[:], 0.0))
@@ -145,8 +148,6 @@ def rank_program(g, core, T, topo):
     v(ts(T.mk[:, 0:1], p8, float(rank), Op.is_equal))
     v(ts(T.mk[:, 1:2], p8, float(rank), Op.not_equal))
     v(ts(T.mk[:, 2:3], p8, float(rank), Op.not_equal))
-    v(V.memset(T.so[:, 8:12], 2.0 ** -120))
-    v(V.memset(T.xo[:, 297:300], 2.0 ** -120))
     vw()
     wait(V, e_u0, e_u1)
     e_uq = ev(V.quantize_mx(T.uq[:], T.uqs[:], T.ut[:]))
@@ -164,7 +165,7 @@ def rank_program(g, core, T, topo):
     wait(V, e_m1)
     e_c1 = ev(V.tensor_copy(T.ck[:, o + 3:o + 5], T.ps[:, 513:515]))
     wait(g, e_c0, e_c1)
-    to_all((T.ck[:, o:o + 5], T.ck[:, o:o + 5]), T.sem.s_ck)
+    to_all(T.ck[:, o:o + 5], T.ck[:, o:o + 5], T.sem.s_ck)
 
     wait(A, e_hz)
     for b in range(4):
@@ -173,125 +174,130 @@ def rank_program(g, core, T, topo):
     aw()
     for b in range(4):
         a(A.activation(T.eb[:, 512 * b + b:512 * b + 512:4], T.ident[:], AF.Copy))
-    e_eb = ev(A.activation(T.h0[:], T.hz[:], AF.Copy))
-    e_eb2 = ev(A.activation(T.h1[:], T.hz[:], AF.Copy))
+    aw()
+    e_eb = ev(A.activation(T["h%d" % mine][:], T.hz[:], AF.Copy))
 
     wait(V, e_hz, e_ones, e_uq, e_t0, e_tr, e_c0, e_c1)
-    mine = [t for t in range(2) if rank in REB[t]][0]
     wait(V, i_rr, i_ir, i_pr, i_x0, i_x1, i_pf, i_kw)
+    v(ts(T.fac[:, 0:32], T.irow[:], p32, Op.is_lt, -2.0 ** -24, Op.mult))
+    v(V.memset(T.fac[:, 32:128], 1.0))
+    v(V.memset(T.g0[:, 130:193], -1.0))
+    v(V.memset(T.g1[:, 130:193], -1.0))
     v(ts(T.wr[:], T.rr[:], -1.0 / 8192, Op.mult, 8.0 / 8192, Op.add))
     v(ts(T.gt[:, 0:8], T.rr[:], p8, Op.not_equal))
     v(ts(T.dm[:], T.rr[:], q1, Op.not_equal))
     v(ts(T.pm[:], T.rr[:], q1, Op.is_equal))
-    v(ts(T.fac[:, 0:32], T.irow[:], p32, Op.is_lt, -2.0 ** -24, Op.mult))
-    v(V.memset(T.fac[:, 32:128], 1.0))
-    v(ts(T.km[:, 0:1], p16, 0.0, Op.add))
-    v(ts(T.km[:, 1:2], p16, 16.0, Op.add))
-    v(ts(T.sel[:, 0:1], p32, 16.0, Op.is_lt))
-    v(ts(T.sel[:, 1:2], p32, 16.0, Op.is_ge))
-    v(ts(T.g0[:, 128:129], T.pf[:], 1.0 / 256, Op.mult))
-    v(ts(T.g1[:, 128:129], T.pf[:], 1.0 / 256, Op.mult))
+    v(ts(T.prb[:], T.pr[:], 127, Op.bitwise_and))
+    v(ts(T.xi[:], T.xr[:], p16, Op.add))
     vw()
-    v(V.tensor_tensor(T.w0[:], T.gt[:, 0:8], T.wr[:], Op.mult))
     v(ts(T.fac[:, 0:32], T.fac[:, 0:32], 1.0, Op.add))
     for b in range(1, 4):
         v(V.memset(T.fac[32 * b:32 * b + 32, 128 - 32 * b:128], 1.0 - 2.0 ** -24))
+    for gg in (T.g0, T.g1):
+        v(V.memset(gg[:, 145:146], 15.0))
+        v(V.memset(gg[:, 177:178], 15.0))
+        v(ts(gg[:, 128:129], T.pf[:], 1.0 / 256, Op.mult))
+    v(V.tensor_tensor(T.w0[:], T.gt[:, 0:8], T.wr[:], Op.mult))
+    v(ts(T.sel[:, 0:1], p32, 16.0, Op.is_lt))
+    v(ts(T.sel[:, 1:2], p32, 16.0, Op.is_ge))
     e_fac = ev(V.memset(T.oz[:, 0:8], 0))
-    v(V.memset(T.oz[:, 8:16], 2))
     vw()
     wait(V, e_fac)
-    v(V.quantize_mx(T["tw0"][:, 0:128], T["tws0"][:, 0:128], T.tbt[:, 0:512]))
     v(V.quantize_mx(T["tw0"][:, 128:256], T["tws0"][:, 128:256], T.hz[:]))
     v(V.quantize_mx(T["la%d" % mine][:, 64:192], T["ls%d" % mine][:, 64:192], T.hz[:]))
     v(V.quantize_mx(T["or%d" % mine][:], T["os%d" % mine][:], T.hz[:]))
     v(V.memset(T.d0[:], 1.0))
-    v(V.memset(T.seg[:], 1.0))
     v(ts(T.lc[:, 0:1], p8, -1.0, Op.add))
     v(ts(T.lc[:, 1:2], p8, 0.0, Op.is_equal))
     v(ts(T.lc[:, 2:3], p16, 8.0, Op.is_lt))
     v(ts(T.lc[:, 3:4], p16, 8.0, Op.is_ge))
+    v(V.tensor_copy(T.c1[:, 0:8], T.prb[:]))
+    v(ts(T.xj[:], T.xi[:], 127, Op.bitwise_and))
     vw()
     v(V.memset(T.d0[:, 0:64:8], 0.0))
     v(V.memset(T.d0[:, 1:64:8], -1.0))
-    v(V.memset(T.seg[:, 0:256:32], 0.0))
-    wait(V, e_eb, e_eb2)
-    e_eq = ev(V.quantize_mx(T.eq[:], T.eqs[:], T.eb[:]))
+    v(ts(T.c1[:, 8:16], T.c1[:, 0:8], 1.0 / 256, Op.mult))
+    v(V.tensor_copy(T.src[:], T.xj[:]))
+    vw()
+    v(V.tensor_tensor(T.c1[:, 0:8], T.c1[:, 8:16], T.wr[:], Op.add))
+    v(ts(T.tgt[:], T.src[:], 1.0 / 256, Op.mult, (8 - rank) / 8192.0, Op.add))
     vw()
     im1, is0, lo8, hi8 = (T.lc[:, i:i + 1] for i in range(4))
 
-    def late_constants():
-        v(ts(T.prb[:], T.pr[:], 127, Op.bitwise_and))
-        v(ts(T.xi[:], T.xr[:], p16, Op.add))
-        vw()
-        v(V.tensor_copy(T.c1[:, 0:8], T.prb[:]))
-        v(ts(T.xj[:], T.xi[:], 127, Op.bitwise_and))
-        vw()
-        v(ts(T.c1[:, 8:16], T.c1[:, 0:8], 1.0 / 256, Op.mult))
-        v(V.tensor_copy(T.src[:], T.xj[:]))
-        vw()
-        v(V.tensor_tensor(T.c1[:, 0:8], T.c1[:, 8:16], T.wr[:], Op.add))
-        v(ts(T.tgt[:], T.src[:], 1.0 / 256, Op.mult, (8 - rank) / 8192.0, Op.add))
-        vw()
+    def unpacker():
+        wait(V, e_eb)
+        e = ev(V.quantize_mx(T.eq[:], T.eqs[:], T.eb[:]))
+        wait(V, e)
+        return e
+
+    if mine == 0:
+        e_eq = unpacker()
+
+    def late():
+        v(V.memset(T.seg[:], 1.0))
+        e3 = ev(V.memset(T.oz[:, 8:16], 2))
         v(V.tensor_tensor(T.c1[:, 8:16], T.c1[:, 0:8], T.pm[:], Op.mult))
+        v(V.quantize_mx(T["tw0"][:, 0:128], T["tws0"][:, 0:128], T.tbt[:, 0:512]))
         vw()
+        wait(V, e3)
+        v(V.memset(T.seg[:, 0:256:32], 0.0))
         v(V.tensor_reduce(T.cf[:, 4:5], T.c1[:, 8:16], X, Op.add))
-        e = ev(V.tensor_copy(T.ur[:, 0:128].bitcast(dt.uint32), T.uq[:, 0:128].bitcast(dt.uint32).indirect(T.oz[:, 0:8])))
-        e2 = ev(V.tensor_copy(T.ur[:, 128:256].bitcast(dt.uint32), T.uq[:, 0:128].bitcast(dt.uint32).indirect(T.oz[:, 8:16])))
-        v(V.quantize_mx(T.wq[:], T.wqs[:], T.wt[:]))
+        e = ev(V.tensor_copy(u32(T.ur[:, 0:128]), u32(T.uq[:, 0:128]).indirect(T.oz[:, 0:8])))
+        e2 = ev(V.tensor_copy(u32(T.ur[:, 128:256]), u32(T.uq[:, 0:128]).indirect(T.oz[:, 8:16])))
         vw()
-        return e, e2
+        return e, e2, e3
 
-    wait(A, e_uq, e_fac)
-    wait(V, e_w)
-    e_ur = late_constants()
-    wait(A, *e_ur)
-    e_us0 = ev(A.activation(T.urs[:, 0:128], T.uqs[:, 0:128].indirect(T.oz[:, 0:8]), AF.Copy))
-    e_us1 = ev(A.activation(T.urs[:, 128:256], T.uqs[:, 0:128].indirect(T.oz[:, 8:16]), AF.Copy))
+    def turn(buf, o, w, n, k):
+        m = (n + k) % 4
+        return buf[32 * n:32 * n + 32, o + k * w:o + k * w + w], buf[32 * m:32 * m + 32, o:o + w]
 
-    def rotate(buf, w):
+    def half(buf, o, w, n):
+        return buf[64 * n:64 * n + 64, o + 2 * w:o + 3 * w], buf[64 - 64 * n:128 - 64 * n, o:o + w]
+
+    def order(t, s, e_s, lost):
+        ex, ar, thr, gg, yo, yb, sm = (T["%s%d" % (n, t)] for n in ("ex", "ar", "thr", "g", "yo", "yb", "sm"))
+        wait(A, e_s, e_fac)
+        e_ex = ev(A.activation(ex[:], T.ones[:, 0:32], AF.Abs, bias=TINY, scale=s))
+        wait(A, e_ex)
+        e_th = ev(A.activation(thr[:], T.fac[:], AF.Copy, scale=ex[:, 0:1]))
+        wait(V, e_s)
+        lost[0]()
+        wait(V, e_ex)
+        e_tp = ev(V.transpose(ar[:, 0:32], ex[:]))
+        vw()
+        lost[1]()
+        wait(V, e_tp)
+        wait(A, e_tp)
         for n in range(4):
-            m = (n + 1) % 4
-            v(V.tensor_copy(buf[32 * n:32 * n + 32, w:2 * w], buf[32 * m:32 * m + 32, 0:w]))
+            v(V.tensor_copy(*turn(ar, 0, 32, n, 1)))
+        v(V.tensor_copy(*half(ar, 0, 32, 0)))
+        v(V.tensor_copy(*half(ar, 0, 32, 1)))
+        for n in range(3):
+            a(A.activation(*turn(ar, 0, 32, n, 3), AF.Copy))
+        aw()
+        e_tn = ev(A.activation(*turn(ar, 0, 32, 3, 3), AF.Copy))
         vw()
-        v(V.tensor_copy(buf[0:64, 2 * w:4 * w], buf[64:128, 0:2 * w]))
-        v(V.tensor_copy(buf[64:128, 2 * w:4 * w], buf[0:64, 0:2 * w]))
-        vw()
-
-    def order(t, s2, lost):
-        ex, ar, thr, gg, yb, sm = (T["%s%d" % (n, t)] for n in ("ex", "ar", "thr", "g", "yb", "sm"))
-        e_a = ev(V.tensor_reduce(sm[:, 0:1], s2, X, Op.max, apply_absolute_value=True))
-        wait(A, e_a, e_fac)
-        e_th = ev(A.activation(thr[:], T.fac[:], AF.Copy, scale=sm[:, 0:1]))
-        wait(V, e_a)
-        v(ts(ex[:, 0:32], T.ones[:, 0:32], sm[:, 0:1], Op.mult))
-        vw()
-        v(V.transpose(ar[:, 0:32], ex[:, 0:32]))
-        vw()
-        rotate(ar, 32)
-        lost()
-        wait(V, e_th)
+        wait(V, e_th, e_tn)
         v(V.tensor_tensor(gg[:, 0:128], ar[:], thr[:], Op.is_gt))
+        lost[2]()
         vw()
-        v(V.tensor_reduce(sm[:, 1:2], gg[:, 0:130], X, Op.add))
+        v(V.tensor_tensor_scan(yo[:], T.ones[:, 0:193], gg[:], 0.0, Op.mult, Op.add))
         vw()
-        v(ts(ex[:, 32:64], T.ones[:, 0:32], sm[:, 1:2], Op.mult))
+        v(V.transpose(yb[:], yo[:, 129:193]))
         vw()
-        v(V.transpose(yb[:, 0:32], ex[:, 32:64]))
-        vw()
-        v(ts(yb[:, 32:64], yb[:, 0:32], T.km[:, 0:1], Op.subtract))
-        v(ts(yb[:, 64:96], yb[:, 0:32], T.km[:, 1:2], Op.subtract))
-        vw()
-        z = sm[:, 8:16]
-        v(V.tensor_reduce(sm[:, 8:9], yb[:, 32:64], X, Op.min, apply_absolute_value=True))
-        v(V.tensor_reduce(sm[:, 9:10], yb[:, 64:96], X, Op.min, apply_absolute_value=True))
-        vw()
+        e_z0 = ev(V.tensor_reduce(sm[:, 8:9], yb[:, 0:32], X, Op.min, apply_absolute_value=True))
+        e_z1 = ev(V.tensor_reduce(sm[:, 9:10], yb[:, 32:64], X, Op.min, apply_absolute_value=True))
+        wait(A, e_z0, e_z1)
+        wait(V, e_z0, e_z1)
         for n in range(4):
-            m = (n + 1) % 4
-            v(V.tensor_copy(sm[32 * n:32 * n + 32, 10:12], sm[32 * m:32 * m + 32, 8:10]))
+            v(V.tensor_copy(*turn(sm, 8, 2, n, 1)))
+        v(V.tensor_copy(*half(sm, 8, 2, 0)))
+        for n in range(4):
+            a(A.activation(*turn(sm, 8, 2, n, 3), AF.Copy))
+        aw()
+        e_zn = ev(A.activation(*half(sm, 8, 2, 1), AF.Copy))
         vw()
-        v(V.tensor_copy(sm[0:64, 12:16], sm[64:128, 8:12]))
-        v(V.tensor_copy(sm[64:128, 12:16], sm[0:64, 8:12]))
-        vw()
+        wait(V, e_zn)
         v(V.tensor_reduce(sm[:, 16:17], sm[:, 8:16:2], X, Op.min))
         v(V.tensor_reduce(sm[:, 17:18], sm[:, 9:16:2], X, Op.min))
         vw()
@@ -303,7 +309,7 @@ def rank_program(g, core, T, topo):
         sc, ss, la, ls = (T["%s%d" % (n, t)] for n in ("sc", "ss", "la", "ls"))
         wait(V, *e_tab)
         wait(A, *e_tab)
-        e_sc = ev(V.tensor_copy(sc[:].bitcast(dt.uint32), tab[:, 0:128].bitcast(dt.uint32).indirect(of[:])))
+        e_sc = ev(V.tensor_copy(u32(sc[:]), u32(tab[:, 0:128]).indirect(of[:])))
         e_ss = ev(A.activation(ss[:], tabs[:, 0:128].indirect(of[:]), AF.Copy))
         sl = slice(NK * rank, NK * rank + NK)
         wait(g, e_sc)
@@ -327,24 +333,21 @@ def rank_program(g, core, T, topo):
         v(V.transpose(vr[:, 32:64], vr[:, 0:32]))
         vw()
         v(ts(vr[:, 64:96], vr[:, 32:64], 256.0, Op.mult))
-        vw()
-        v(V.tensor_copy(vi[:, 0:32], vr[:, 64:96]))
+        v(ts(vi[:, 0:32], vr[:, 32:64], 256.0, Op.mult))
+        v(ts(vi[:, 32:64], vr[:, 32:64], 256.0, Op.mult, float(t), Op.add))
         vw()
         v(V.tensor_copy(bsb[:, 0:32], vi[:, 0:32]))
-        v(ts(vi[:, 32:64], vi[:, 0:32], t, Op.add))
-        vw()
-        v(V.tensor_tensor(vr[:, 96:128], vr[:, 64:96], bsb[:, 0:32], Op.subtract))
         v(ts(vi[:, 64:96], vi[:, 32:64], 7, Op.bitwise_and))
         vw()
-        e_b = ev(ts(bsb[:, 32:64], vr[:, 96:128], -32.0, Op.mult, 8.0, Op.add))
+        v(V.tensor_tensor(vr[:, 96:128], vr[:, 64:96], bsb[:, 0:32], Op.subtract))
         v(V.tensor_copy(vr[:, 128:160], vi[:, 64:96]))
         vw()
-        wait(V, e_b)
+        e_b = ev(ts(bsb[:, 32:64], vr[:, 96:128], -32.0, Op.mult, 8.0, Op.add))
         wait(SY, e_b)
         fin.append(ev(SY.dma_start(T.bs[2 * t:2 * t + 2, 0:32], bsb[0:1, 0:64]), 16))
-        return own
+        return own, e_b
 
-    def rebuild_list(t):
+    def rebuild_list(t, e_b):
         s = NK * REB[t].index(rank)
         vr, bsb, rl, ol = T["vr%d" % t], T["bsb%d" % t], T["rl%d" % t], T["ol%d" % t]
         q, lost = vr[:, 128 + s:136 + s], bsb[:, 32 + s:40 + s]
@@ -353,6 +356,7 @@ def rank_program(g, core, T, topo):
         vw()
         v(V.tensor_tensor(rl[:, 16:24], rl[:, 0:8], rl[:, 8:16], Op.max))
         vw()
+        wait(V, e_b)
         v(V.tensor_tensor(rl[:, 24:32], rl[:, 16:24], lost, Op.is_equal))
         v(ts(rl[:, 32:40], rl[:, 16:24], float(NK), Op.mult))
         vw()
@@ -374,31 +378,35 @@ def rank_program(g, core, T, topo):
         la, ls, od, os_, h, nq, ns, sb, ol = (T["%s%d" % (n, t)] for n in ("la", "ls", "or", "os", "h", "nq", "ns", "sb", "ol"))
         D = T.da if t == 0 else T.db
         arr = (T.sem["s_la%d" % t], 7 * 2 * (EW // 4))
-        wait(V, arr, *own)
-        e_oc = ev(V.tensor_copy(od[:, 0:64].bitcast(dt.uint32), la[:, 0:96].bitcast(dt.uint32).indirect(ol[:])))
-        wait(A, e_ol, arr, *own)
+        wait(V, *own)
+        wait(V, arr)
+        e_oc = ev(V.tensor_copy(u32(od[:, 0:64]), u32(la[:, 0:96]).indirect(ol[:])))
+        wait(A, e_ol, *own)
+        wait(A, arr)
         e_os = ev(A.activation(os_[:, 0:64], ls[:, 0:96].indirect(ol[:]), AF.Copy))
         wait(PE, e_eq, e_oc, e_os)
-        scans = []
+        scans, cps = [], []
         for b in range(4):
             k = 512 * (b % 3)
             if b == 3:
                 wait(PE, scans[0])
             e_d = ev(PE.matmul_mx(D[:, k:k + 128], T.eq[:, 128 * b:128 * b + 128], T.eqs[:, 128 * b:128 * b + 128], od[:], os_[:], True, True))
             wait(V, e_d)
-            e = ev(V.tensor_tensor_scan(sb[:, 64 * b:64 * b + 64], T.d0[:], D[:, k:k + 64], 0.0, Op.mult, Op.subtract))
-            scans.append(e)
-            wait(V, e)
-            v(V.tensor_copy(h[:, b:4 * NK:4], sb[:, 64 * b + 7:64 * b + 64:8]))
-        vw()
+            scans.append(ev(V.tensor_tensor_scan(sb[:, 64 * b:64 * b + 64], T.d0[:], D[:, k:k + 64], 0.0, Op.mult, Op.subtract)))
+        for b in range(3):
+            wait(A, scans[b])
+            cps.append(ev(A.activation(h[:, b:4 * NK:4], sb[:, 64 * b + 7:64 * b + 64:8], AF.Copy)))
+        wait(V, scans[3])
+        cps.append(ev(V.tensor_copy(h[:, 3:4 * NK:4], sb[:, 199:256:8])))
+        wait(V, e_eb, *scans)
+        wait(V, *cps)
         e_nq = ev(V.quantize_mx(nq[:], ns[:], h[:]))
-        wait(V, e_nq)
         i = REB[t].index(rank)
         sl = slice(P + NK * i, P + NK * i + NK)
         tw, tws = T["tw%d" % t], T["tws%d" % t]
         wait(g, e_nq)
-        to_all((u8(nq[:, 0:NK]), u8(tw[:, sl])), T.sem["s_nw%d" % t])
-        to_all((ns[:, 0:NK], tws[:, sl]), T.sem["s_nw%d" % t])
+        to_all(u8(nq[:, 0:NK]), u8(tw[:, sl]), T.sem["s_nw%d" % t])
+        to_all(ns[:, 0:NK], tws[:, sl], T.sem["s_nw%d" % t])
         wait(SY, e_nq)
         return [ev(SY.dma_start(u8(tw[:, sl]), u8(nq[:, 0:NK])), 16), ev(SY.dma_start(tws[:, sl], ns[:, 0:NK]), 16)]
 
@@ -417,42 +425,47 @@ def rank_program(g, core, T, topo):
         wait(V, e)
         return e
 
+    def arrived(t):
+        return (T.sem["s_nw%d" % t], EW * (6 if mine == t else 8))
+
     s_ck = (T.sem.s_ck, 7 * EW)
-    wait(A, s_ck, e_c0, e_c1)
+    wait(A, e_c0, e_c1)
+    wait(A, s_ck)
     e_ag0 = ev(A.activation(T.ag[:, 0:8], T.ck[:, 2:64:8], AF.Abs))
     e_ag1 = ev(A.activation(T.ag[:, 8:16], T.ck[:, 4:64:8], AF.Abs))
     wait(V, s_ck)
     v(V.tensor_reduce(T.cf[:, 5:6], T.ck[:, 0:64:8], X, Op.add))
     vw()
-    v(V.tensor_tensor_scan(T.so[:, 0:8], T.ones[:, 0:8], T.ck[:, 1:64:8], T.cf[:, 5:6], Op.mult, Op.subtract))
-    vw()
+    e_s = ev(V.tensor_tensor_scan(T.so[:, 0:8], T.ones[:, 0:8], T.ck[:, 1:64:8], T.cf[:, 5:6], Op.mult, Op.subtract))
 
-    def lost0():
+    def l0a():
         wait(V, e_ag0)
         v(V.tensor_reduce(T.cf[:, 6:7], T.ag[:, 0:8], X, Op.max))
         vw()
         v(ts(T.gt[:, 8:16], T.ag[:, 0:8], T.cf[:, 6:7], Op.is_equal))
-        vw()
-        v(V.tensor_tensor(T.gt[:, 16:24], T.gt[:, 8:16], T.w0[:], Op.mult))
-        vw()
-        v(V.tensor_reduce(T.g0[:, 129:130], T.gt[:, 16:24], X, Op.max))
-        vw()
 
-    own = order(0, T.so[:, 7:9], lost0)
+    def l0b():
+        v(V.tensor_tensor(T.gt[:, 16:24], T.gt[:, 8:16], T.w0[:], Op.mult))
+
+    def l0c():
+        v(V.tensor_reduce(T.g0[:, 129:130], T.gt[:, 16:24], X, Op.max))
+
+    own, e_b = order(0, T.so[:, 7:8], e_s, (l0a, l0b, l0c))
+    new_own = []
     if mine == 0:
-        e_ol = rebuild_list(0)
+        e_ol = rebuild_list(0, e_b)
+        new_own = rebuild(0, own, e_ol)
+    wait(V, e_b)
+    e_ur0, e_ur1, e_oz = late()
+    wait(A, e_uq, e_fac, e_ur0, e_ur1, e_oz)
+    e_us0 = ev(A.activation(T.urs[:, 0:128], T.uqs[:, 0:128].indirect(T.oz[:, 0:8]), AF.Copy))
+    e_us1 = ev(A.activation(T.urs[:, 128:256], T.uqs[:, 0:128].indirect(T.oz[:, 8:16]), AF.Copy))
     codeq = T.cf[:, 4:5]
     vr = T["vr0"]
     e_ms = []
     for r in range(N):
         e_ms.append(ev(ts(T.msk[:, 32 * r:32 * r + 32], vr[:, 32:64], T.c1[:, r:r + 1], Op.is_equal, T.dm[:, r:r + 1], Op.mult)))
     e_ms.append(ev(ts(T.msk[:, 256:288], vr[:, 32:64], codeq, Op.is_equal, -1.0, Op.mult)))
-    new_own = []
-    if mine == 0:
-        wait(V, *e_ms)
-        new_own = rebuild(0, own, e_ol)
-    else:
-        wait(V, *e_ms)
     for r in range(N + 1):
         wait(A, e_ms[r])
         if r:
@@ -460,26 +473,28 @@ def rank_program(g, core, T, topo):
         a(A.activation(T.junk[:], T.msk[:, 32 * r:32 * r + 32], AF.Copy, accum_out=T.rep[:, r:r + 1]))
     aw()
     e_rep = ev(A.activation(T.gt[:, 64:72], T.rep[:, 0:8], AF.Copy))
+    e_oi = table_list(0)
+    wait(V, *e_ms)
     hit, hi = T.hit, T.hiti
     bsb = T["bsb0"]
     v(V.tensor_tensor(hit[:, 0:32], bsb[:, 0:32], bsb[:, 32:64], Op.subtract))
-    v(ts(hit[:, 32:64], bsb[:, 32:64], q1, Op.not_equal))
     v(V.tensor_tensor(T.gt[:, 24:32], T.ck[:, 3:64:8], T.pm[:], Op.mult))
+    v(ts(hit[:, 32:64], bsb[:, 32:64], q1, Op.not_equal))
     vw()
     v(ts(hi[:, 0:32], hit[:, 0:32], 128.0, Op.add))
     v(V.tensor_reduce(T.cf[:, 7:8], T.gt[:, 24:32], X, Op.add))
-    vw()
-    v(ts(hi[:, 32:64], hi[:, 0:32], 127, Op.bitwise_and))
     wait(V, e_rep)
     v(V.tensor_tensor(T.gt[:, 32:40], T.dm[:], T.gt[:, 64:72], Op.subtract))
     v(ts(T.gt[:, 40:41], T.rep[:, 8:9], 1.0, Op.add, -1.0, Op.mult))
     vw()
-    v(V.tensor_copy(hit[:, 64:96], hi[:, 32:64]))
+    v(ts(hi[:, 32:64], hi[:, 0:32], 127, Op.bitwise_and))
     v(V.tensor_tensor(T.xs[:, 65:297:33], T.ck[:, 3:64:8], T.gt[:, 32:40], Op.mult))
+    v(V.tensor_tensor(T.xs[:, 32:33], T.cf[:, 7:8], T.gt[:, 40:41], Op.mult))
     v(V.tensor_tensor(T.w40[:, 0:8], T.gt[:, 32:40], T.wr[:], Op.mult))
     wait(V, e_ag1)
     v(V.tensor_tensor(T.gv[:, 0:8], T.gt[:, 32:40], T.ag[:, 8:16], Op.mult))
-    v(V.tensor_tensor(T.xs[:, 32:33], T.cf[:, 7:8], T.gt[:, 40:41], Op.mult))
+    vw()
+    v(V.tensor_copy(hit[:, 64:96], hi[:, 32:64]))
     vw()
     v(ts(hit[:, 96:128], hit[:, 64:96], T.pf[:, 0:1], Op.is_equal))
     vw()
@@ -489,19 +504,18 @@ def rank_program(g, core, T, topo):
     vw()
     v(ts(T.w40[:, 8:40], hit[:, 0:32], 1.0 / 256, Op.mult))
     vw()
-    e_oi = table_list(0)
 
-    def arrived(t):
-        return (T.sem["s_nw%d" % t], 2 * EW * (4 - (1 if mine == t else 0)))
     nw = arrived(0)
-    wait(PE, nw, *new_own)
-    wait(PE, e_us0, e_us1, *e_ur)
-    wait(PE, e_c0, e_c1)
+    wait(PE, e_us0, e_us1, e_ur0, e_ur1)
+    wait(PE, e_c0, e_c1, *new_own)
+    wait(PE, nw)
     e_cn = ev(PE.matmul_mx(T.ps[:, 0:128], T.ur[:, 0:128], T.urs[:, 0:128], T["tw0"][:, 128:256], T["tws0"][:, 128:256], True, True))
     e_gn = ev(PE.matmul_mx(T.ps[:, 512:640], T.ur[:, 128:256], T.urs[:, 128:256], T["tw0"][:, 128:256], T["tws0"][:, 128:256], True, True))
-    wait(V, nw, *new_own)
-    p1 = ev(V.tensor_copy(T.t1[:].bitcast(dt.uint32), T["tw0"][:, 0:160].bitcast(dt.uint32).indirect(T.oi0[:])))
-    wait(A, nw, e_oi, *new_own)
+    wait(V, *new_own)
+    wait(V, nw)
+    p1 = ev(V.tensor_copy(u32(T.t1[:]), u32(T["tw0"][:, 0:160]).indirect(T.oi0[:])))
+    wait(A, e_oi, *new_own)
+    wait(A, nw)
     p2 = ev(A.activation(T.t1s[:], T["tws0"][:, 0:160].indirect(T.oi0[:]), AF.Copy))
     e_t1 = [p1, p2]
     wait(A, e_gn)
@@ -516,41 +530,48 @@ def rank_program(g, core, T, topo):
     e_xp = ev(V.tensor_tensor(T.xs[:, 33 + 33 * r:65 + 33 * r], T.msk[:, 32 * r:32 * r + 32], T.ps[:, 0:32], Op.mult))
     vw()
     wait(V, e_xp)
-    v(V.tensor_tensor_scan(T.xo[:, 0:297], T.ones[:, 0:297], T.xs[:, 0:297], 0.0, Op.mult, Op.subtract))
-    vw()
+    e_s = ev(V.tensor_tensor_scan(T.xo[:, 0:297], T.ones[:, 0:297], T.xs[:, 0:297], 0.0, Op.mult, Op.subtract))
 
-    def lost1():
+    def l1a():
         wait(V, e_agn)
         v(V.tensor_tensor(T.gv[:, 8:40], T.agn[:], hit[:, 128:160], Op.mult))
         vw()
         v(V.tensor_reduce(T.gt[:, 42:43], T.gv[:], X, Op.max))
-        vw()
-        v(ts(T.ex0[:, 0:40], T.gv[:], T.gt[:, 42:43], Op.is_equal))
-        vw()
-        v(V.tensor_tensor(T.yb0[:, 0:40], T.ex0[:, 0:40], T.w40[:], Op.mult))
-        vw()
-        v(V.tensor_reduce(T.g1[:, 129:130], T.yb0[:, 0:40], X, Op.max))
-        vw()
 
-    own = order(1, T.xo[:, 296:298], lost1)
-    new_own = []
+    def l1b():
+        v(ts(T.lw[:, 0:40], T.gv[:], T.gt[:, 42:43], Op.is_equal))
+        vw()
+        v(V.tensor_tensor(T.lw[:, 40:80], T.lw[:, 0:40], T.w40[:], Op.mult))
+
+    def l1c():
+        v(V.tensor_reduce(T.g1[:, 129:130], T.lw[:, 40:80], X, Op.max))
+
+    own, e_b = order(1, T.xo[:, 296:297], e_s, (l1a, l1b, l1c))
     if mine == 1:
-        e_ol = rebuild_list(1)
+        e_ol = rebuild_list(1, e_b)
+        e_eq = unpacker()
         new_own = rebuild(1, own, e_ol)
+    else:
+        new_own = []
+    wait(V, e_b)
     e_oi = table_list(1)
+    wait(V, e_w, e_eb)
+    e_wq = ev(V.quantize_mx(T.wq[:], T.wqs[:], T.wt[:]))
     nw = arrived(1)
-    wait(V, nw, *new_own)
     wait(V, *e_tw)
-    p1 = ev(V.tensor_copy(T.t2[:].bitcast(dt.uint32), T["tw1"][:, 0:160].bitcast(dt.uint32).indirect(T.oi1[:])))
-    wait(A, nw, e_oi, *new_own)
-    wait(A, *e_tw)
+    wait(V, *new_own)
+    wait(V, nw)
+    p1 = ev(V.tensor_copy(u32(T.t2[:]), u32(T["tw1"][:, 0:160]).indirect(T.oi1[:])))
+    wait(A, e_oi, *e_tw)
+    wait(A, *new_own)
+    wait(A, nw)
     p2 = ev(A.activation(T.t2s[:], T["tws1"][:, 0:160].indirect(T.oi1[:]), AF.Copy))
     wait(SY, p1)
     fin.append(ev(SY.dma_start(T.oc[:, 0:512], u8(T.t2[:])), 16))
     wait(A, p2)
     for k in range(4):
         fin.append(ev(A.dma_start(T.osc[4 * k:4 * k + 4, 0:128], T.t2s[32 * k:32 * k + 4, 0:128]), 16))
-    wait(PE, p1, p2, e_xp)
+    wait(PE, e_wq, e_xp, p1, p2)
     e_y = ev(PE.matmul_mx(T.ps[:, 0:128], T.wq[:], T.wqs[:], T.t2[:], T.t2s[:], True, True))
     wait(V, e_y)
     e_yc = ev(V.tensor_copy(T.ysb[:], T.ps[:, 0:128]))

@@ -20,27 +20,27 @@ SCRATCH = {
     "eq": _sb(512, X4), "eqs": _sb(512, U8),
     "ur": _sb(256, X4), "urs": _sb(256, U8),
     "t1": _sb(128, X4), "t1s": _sb(128, U8), "t2": _sb(128, X4), "t2s": _sb(128, U8),
-    "ones": _sb(304, F32), "ident": _sb(128, F32), "ck": _sb(64, F32),
+    "ones": _sb(256, F32), "ident": _sb(128, F32), "ck": _sb(576, F32), "dz": _sb(361, F32),
     "pi": _sb(2, I32), "pj": _sb(4, I32), "cf": _sb(8, F32), "mk": _sb(4, F32), "rr": _sb(8, F32), "irow": _sb(32, F32),
     "pr": _sb(8, I32), "prb": _sb(8, I32), "xr": _sb(16, F32), "xi": _sb(16, I32), "xj": _sb(16, I32), "kw": _sb(256, F32), "pf": _sb(1, F32),
-    "sel": _sb(2, F32), "wr": _sb(8, F32), "w0": _sb(8, F32), "dm": _sb(8, F32), "pm": _sb(8, F32),
-    "c1": _sb(16, F32), "src": _sb(16, F32), "tgt": _sb(16, F32), "lc": _sb(4, F32), "fac": _sb(128, F32), "seg": _sb(256, F32),
+    "wr": _sb(8, F32), "w32": _sb(8, F32), "w0": _sb(8, F32), "dm": _sb(8, F32), "pm": _sb(8, F32), "c1": _sb(24, F32),
+    "src": _sb(16, F32), "tgt": _sb(16, F32), "lc": _sb(8, F32), "rm": _sb(8, F32), "kb": _sb(8, F32), "fac": _sb(128, F32), "seg": _sb(256, F32),
     "d0": _sb(64, F32), "oz": _sb(16, U16),
-    "ag": _sb(16, F32), "agn": _sb(32, F32), "so": _sb(12, F32), "xo": _sb(300, F32), "xs": _sb(300, F32), "msk": _sb(288, F32),
-    "rep": _sb(9, F32), "junk": _sb(32, F32), "hit": _sb(160, F32), "hiti": _sb(64, I32), "gv": _sb(40, F32), "w40": _sb(40, F32), "gt": _sb(96, F32),
+    "ag": _sb(16, F32), "agn": _sb(32, F32), "so": _sb(72, F32), "xo": _sb(361, F32), "xs": _sb(361, F32), "msk": _sb(288, F32),
+    "rep": _sb(9, F32), "junk": _sb(288, F32), "hit": _sb(192, F32), "hiti": _sb(64, I32), "gv": _sb(40, F32), "w40": _sb(40, F32), "gt": _sb(96, F32),
     "lw": _sb(96, F32), "ysb": _sb(128, F32),
-    "ps": ("psum", [128, 1024], F32), "da": ("psum", [128, 1536], F32), "db": ("psum", [128, 1536], F32),
+    "ps": ("psum", [128, 512], F32), "da": ("psum", [128, 2048], F32), "db": ("psum", [128, 1536], F32),
 }
 for _t in "01":
     SCRATCH.update({
         "sc" + _t: _sb(32, X4), "ss" + _t: _sb(32, U8), "la" + _t: _sb(192, X4), "ls" + _t: _sb(192, U8),
         "or" + _t: _sb(128, X4), "os" + _t: _sb(128, U8), "h" + _t: _sb(512, BF), "nq" + _t: _sb(128, X4), "ns" + _t: _sb(128, U8),
         "tw" + _t: _sb(256, X4), "tws" + _t: _sb(256, U8), "sb" + _t: _sb(256, F32),
-        "ex" + _t: _sb(32, F32), "ar" + _t: _sb(128, F32), "thr" + _t: _sb(128, F32), "g" + _t: _sb(193, F32), "yo" + _t: _sb(193, F32),
-        "yb" + _t: _sb(64, F32), "sm" + _t: _sb(32, F32), "of" + _t: _sb(2, U16), "vr" + _t: _sb(192, F32), "vi" + _t: _sb(96, I32),
+        "sr" + _t: _sb(64, F32), "ar" + _t: _sb(128, F32), "thr" + _t: _sb(128, F32), "g" + _t: _sb(193, F32), "yo" + _t: _sb(193, F32),
+        "yb" + _t: _sb(64, F32), "sm" + _t: _sb(32, F32), "of" + _t: _sb(2, U16), "vx" + _t: _sb(128, F32), "vr" + _t: _sb(96, F32), "vi" + _t: _sb(96, I32),
         "bsb" + _t: _sb(64, F32), "rl" + _t: _sb(96, F32), "ol" + _t: _sb(4, U16), "ei" + _t: _sb(784, F32), "oi" + _t: _sb(8, U16),
     })
-SEMAPHORES = ["v", "a", "sl", "s_ck", "s_la0", "s_la1", "s_nw0", "s_nw1"] + ["e%d" % _i for _i in range(130)]
+SEMAPHORES = ["v", "a", "sl", "s_ck", "s_la0", "s_la1", "s_nw0", "s_nw1"] + ["e%d" % _i for _i in range(135)]
 
 
 def rank_program(g, core, T, topo):
@@ -80,6 +80,9 @@ def rank_program(g, core, T, topo):
             return V.tensor_scalar(out, i0, s1, None, op0)
         return V.tensor_scalar(out, i0, s1, s2, op0, op1)
 
+    def tt(out, i0, i1, op):
+        return V.tensor_tensor(out, i0, i1, op)
+
     def u8(view):
         return view.bitcast(dt.uint8)
 
@@ -113,10 +116,9 @@ def rank_program(g, core, T, topo):
     mine = [t for t in range(2) if rank in REB[t]][0]
 
     e_tb = ev(SY.dma_start(T.tbt[:, 0:512], T.tb[:, 0:512]), 16)
+    e_tb2 = ev(A.dma_start(T.tbt[:, 512:544], T.tb[:, 0:32]), 16)
     e_u0 = ev(A.dma_start(T.ut[:, 0:4], T.u[:, 0:4]), 16)
     e_u1 = ev(A.dma_start(T.ut[:, 4:16], T.u[:, 0:12]), 16)
-    e_tb2 = ev(SY.dma_start(T.tbt[:, 512:544], T.tb[:, 0:32]), 16)
-    e_w = ev(SY.dma_start(T.wt[:], T.w[:, 0:512]), 16)
 
     def iota(out, pat, base, cm, f=True):
         if f:
@@ -137,18 +139,17 @@ def rank_program(g, core, T, topo):
     e_id = ev(g.affine_select(T.ident[:], T.ones[:, 0:128], [[-1, 128]], Op.is_equal, 0.0, 0, 1))
     i_kw = iota(T.kw[:, 0:256], [[0, 8], [1, 32]], P, 0)
     wait(V, i_pi)
+    v(ts(T.pj[:, 2:3], T.pi[:, 0:1], 7, Op.bitwise_and))
     v(ts(T.pj[:, 0:1], T.pi[:, 0:1], 15, Op.bitwise_and))
     v(ts(T.pj[:, 1:2], T.pi[:, 0:1], 31, Op.bitwise_and))
-    v(ts(T.pj[:, 2:3], T.pi[:, 0:1], 7, Op.bitwise_and))
     v(ts(T.pj[:, 3:4], T.pi[:, 1:2], 7, Op.bitwise_and))
     vw()
+    v(ts(T.mk[:, 0:1], T.pj[:, 2:3], float(rank), Op.is_equal))
+    v(ts(T.mk[:, 1:2], T.pj[:, 2:3], float(rank), Op.not_equal))
+    v(ts(T.mk[:, 2:3], T.pj[:, 2:3], float(rank), Op.not_equal))
     v(V.tensor_copy(T.cf[:, 0:4], T.pj[:, 0:4]))
     vw()
     p16, p32, p8, q1 = (T.cf[:, i:i + 1] for i in range(4))
-    v(ts(T.mk[:, 0:1], p8, float(rank), Op.is_equal))
-    v(ts(T.mk[:, 1:2], p8, float(rank), Op.not_equal))
-    v(ts(T.mk[:, 2:3], p8, float(rank), Op.not_equal))
-    vw()
     wait(V, e_u0, e_u1)
     e_uq = ev(V.quantize_mx(T.uq[:], T.uqs[:], T.ut[:]))
     wait(V, e_tb)
@@ -158,38 +159,54 @@ def rank_program(g, core, T, topo):
     wait(PE, e_uq, e_t0)
     e_m0 = ev(PE.matmul_mx(T.ps[:, 0:128], T.t0[:], T.t0s[:], T.uq[:], T.uqs[:], True, True))
     wait(PE, e_tr)
-    e_m1 = ev(PE.matmul_mx(T.ps[:, 512:640], T.tr[:], T.trs[:], T.uq[:], T.uqs[:], True, True))
+    e_m1 = ev(PE.matmul_mx(T.db[:, 0:128], T.tr[:], T.trs[:], T.uq[:], T.uqs[:], True, True))
     o = 8 * rank
     wait(V, e_m0)
-    e_c0 = ev(V.tensor_tensor(T.ck[:, o:o + 3], T.ps[:, 0:3], T.mk[:, 0:3], Op.mult))
+    e_c0 = ev(tt(T.ck[:, o:o + 3], T.ps[:, 0:3], T.mk[:, 0:3], Op.mult))
     wait(V, e_m1)
-    e_c1 = ev(V.tensor_copy(T.ck[:, o + 3:o + 5], T.ps[:, 513:515]))
+    e_c1 = ev(V.tensor_copy(T.ck[:, o + 3:o + 5], T.db[:, 1:3]))
     wait(g, e_c0, e_c1)
     to_all(T.ck[:, o:o + 5], T.ck[:, o:o + 5], T.sem.s_ck)
+    wait(SY, e_t0)
+    e_tw0 = [ev(SY.dma_start(u8(T.tw0[:, 0:128]), u8(T.t0[:])), 16), ev(SY.dma_start(T.tws0[:, 0:128], T.t0s[:]), 16)]
+    e_w = ev(SY.dma_start(T.wt[:], T.w[:, 0:512]), 16)
 
-    wait(A, e_hz)
+    wait(A, e_hz, e_ones)
+    e_k0 = ev(A.activation(T.ck[:, 72:576], T.hz[:, 0:504], AF.Copy))
+    e_k1 = ev(A.activation(T.dz[:, 0:256], T.ones[:], AF.Copy))
+    e_k2 = ev(A.activation(T.dz[:, 256:361], T.ones[:, 0:105], AF.Copy))
     for b in range(4):
         a(A.activation(T.eb[:, 512 * b:512 * b + 512], T.hz[:], AF.Copy))
+    e_k3 = ev(A.activation(T.d0[:], T.ones[:, 0:64], AF.Copy))
     wait(A, e_id)
     aw()
     for b in range(4):
         a(A.activation(T.eb[:, 512 * b + b:512 * b + 512:4], T.ident[:], AF.Copy))
+    a(A.activation(T.seg[:], T.ones[:], AF.Copy))
     aw()
+    e_seg = ev(A.activation(T.seg[:, 0:256:32], T.hz[:, 0:8], AF.Copy))
     e_eb = ev(A.activation(T["h%d" % mine][:], T.hz[:], AF.Copy))
 
     wait(V, e_hz, e_ones, e_uq, e_t0, e_tr, e_c0, e_c1)
     wait(V, i_rr, i_ir, i_pr, i_x0, i_x1, i_pf, i_kw)
     v(ts(T.fac[:, 0:32], T.irow[:], p32, Op.is_lt, -2.0 ** -24, Op.mult))
     v(V.memset(T.fac[:, 32:128], 1.0))
+    v(V.memset(T.ck[:, 64:72], -TINY))
+    v(V.memset(T.xs[:, 297:298], -TINY))
+    v(V.memset(T.xs[:, 298:361], 0.0))
     v(V.memset(T.g0[:, 130:193], -1.0))
     v(V.memset(T.g1[:, 130:193], -1.0))
     v(ts(T.wr[:], T.rr[:], -1.0 / 8192, Op.mult, 8.0 / 8192, Op.add))
+    v(ts(T.w32[:], T.rr[:], -1.0 / 32, Op.mult, 8.0 / 32, Op.add))
     v(ts(T.gt[:, 0:8], T.rr[:], p8, Op.not_equal))
-    v(ts(T.dm[:], T.rr[:], q1, Op.not_equal))
-    v(ts(T.pm[:], T.rr[:], q1, Op.is_equal))
     v(ts(T.prb[:], T.pr[:], 127, Op.bitwise_and))
     v(ts(T.xi[:], T.xr[:], p16, Op.add))
+    v(ts(T.lc[:, 6:7], p16, 8.0, Op.is_ge, -1000.0, Op.mult))
+    v(ts(T.lc[:, 7:8], p16, 8.0, Op.is_lt, -1000.0, Op.mult))
+    v(ts(T.dm[:], T.rr[:], q1, Op.not_equal))
+    v(ts(T.pm[:], T.rr[:], q1, Op.is_equal))
     vw()
+    wait(V, e_k0, e_k1, e_k2)
     v(ts(T.fac[:, 0:32], T.fac[:, 0:32], 1.0, Op.add))
     for b in range(1, 4):
         v(V.memset(T.fac[32 * b:32 * b + 32, 128 - 32 * b:128], 1.0 - 2.0 ** -24))
@@ -197,55 +214,38 @@ def rank_program(g, core, T, topo):
         v(V.memset(gg[:, 145:146], 15.0))
         v(V.memset(gg[:, 177:178], 15.0))
         v(ts(gg[:, 128:129], T.pf[:], 1.0 / 256, Op.mult))
-    v(V.tensor_tensor(T.w0[:], T.gt[:, 0:8], T.wr[:], Op.mult))
-    v(ts(T.sel[:, 0:1], p32, 16.0, Op.is_lt))
-    v(ts(T.sel[:, 1:2], p32, 16.0, Op.is_ge))
-    e_fac = ev(V.memset(T.oz[:, 0:8], 0))
-    vw()
-    wait(V, e_fac)
-    v(V.quantize_mx(T["tw0"][:, 128:256], T["tws0"][:, 128:256], T.hz[:]))
-    v(V.quantize_mx(T["la%d" % mine][:, 64:192], T["ls%d" % mine][:, 64:192], T.hz[:]))
-    v(V.quantize_mx(T["or%d" % mine][:], T["os%d" % mine][:], T.hz[:]))
-    v(V.memset(T.d0[:], 1.0))
+    v(V.memset(T.dz[:, 329:330], -1.0))
+    v(tt(T.w0[:], T.gt[:, 0:8], T.wr[:], Op.mult))
+    v(ts(T.rm[:, 0:8:2], T.rr[:, 0:8:2], T.lc[:, 6:7], Op.add))
+    v(ts(T.rm[:, 1:8:2], T.rr[:, 1:8:2], T.lc[:, 7:8], Op.add))
     v(ts(T.lc[:, 0:1], p8, -1.0, Op.add))
-    v(ts(T.lc[:, 1:2], p8, 0.0, Op.is_equal))
-    v(ts(T.lc[:, 2:3], p16, 8.0, Op.is_lt))
-    v(ts(T.lc[:, 3:4], p16, 8.0, Op.is_ge))
+    v(ts(T.lc[:, 1:2], p8, 0.0, Op.is_equal, 8.0, Op.mult))
+    v(ts(T.lc[:, 2:3], p16, 8.0, Op.is_lt, 64.0, Op.mult))
+    v(ts(T.lc[:, 3:4], p16, 8.0, Op.is_ge, 64.0, Op.mult))
+    v(ts(T.lc[:, 4:5], p8, -1.0, Op.add, 8.0, Op.mult))
     v(V.tensor_copy(T.c1[:, 0:8], T.prb[:]))
     v(ts(T.xj[:], T.xi[:], 127, Op.bitwise_and))
+    v(V.memset(T.oz[:, 0:8], 0))
+    v(V.memset(T.oz[:, 8:16], 2))
+    e_fac = ev(V.quantize_mx(T.tw0[:, 128:256], T.tws0[:, 128:256], T.hz[:]))
     vw()
+    wait(V, e_fac, e_k3)
+    v(ts(T.kb[:], T.rm[:], T.lc[:, 4:5], Op.add))
     v(V.memset(T.d0[:, 0:64:8], 0.0))
     v(V.memset(T.d0[:, 1:64:8], -1.0))
-    v(ts(T.c1[:, 8:16], T.c1[:, 0:8], 1.0 / 256, Op.mult))
     v(V.tensor_copy(T.src[:], T.xj[:]))
+    e_oz = ev(tt(T.c1[:, 8:16], T.c1[:, 0:8], T.w32[:], Op.add))
+    v(V.quantize_mx(T["la%d" % mine][:, 64:192], T["ls%d" % mine][:, 64:192], T.hz[:]))
+    v(V.quantize_mx(T["or%d" % mine][:], T["os%d" % mine][:], T.hz[:]))
     vw()
-    v(V.tensor_tensor(T.c1[:, 0:8], T.c1[:, 8:16], T.wr[:], Op.add))
-    v(ts(T.tgt[:], T.src[:], 1.0 / 256, Op.mult, (8 - rank) / 8192.0, Op.add))
-    vw()
-    im1, is0, lo8, hi8 = (T.lc[:, i:i + 1] for i in range(4))
+    wait(V, e_oz)
+    v(ts(T.tgt[:], T.src[:], (8 - rank) / 32.0, Op.add))
+    v(tt(T.c1[:, 16:24], T.c1[:, 8:16], T.pm[:], Op.mult))
+    im1, is08, lo64, hi64 = (T.lc[:, i:i + 1] for i in range(4))
 
     def unpacker():
         wait(V, e_eb)
-        e = ev(V.quantize_mx(T.eq[:], T.eqs[:], T.eb[:]))
-        wait(V, e)
-        return e
-
-    if mine == 0:
-        e_eq = unpacker()
-
-    def late():
-        v(V.memset(T.seg[:], 1.0))
-        e3 = ev(V.memset(T.oz[:, 8:16], 2))
-        v(V.tensor_tensor(T.c1[:, 8:16], T.c1[:, 0:8], T.pm[:], Op.mult))
-        v(V.quantize_mx(T["tw0"][:, 0:128], T["tws0"][:, 0:128], T.tbt[:, 0:512]))
-        vw()
-        wait(V, e3)
-        v(V.memset(T.seg[:, 0:256:32], 0.0))
-        v(V.tensor_reduce(T.cf[:, 4:5], T.c1[:, 8:16], X, Op.add))
-        e = ev(V.tensor_copy(u32(T.ur[:, 0:128]), u32(T.uq[:, 0:128]).indirect(T.oz[:, 0:8])))
-        e2 = ev(V.tensor_copy(u32(T.ur[:, 128:256]), u32(T.uq[:, 0:128]).indirect(T.oz[:, 8:16])))
-        vw()
-        return e, e2, e3
+        return ev(V.quantize_mx(T.eq[:], T.eqs[:], T.eb[:]))
 
     def turn(buf, o, w, n, k):
         m = (n + k) % 4
@@ -254,34 +254,38 @@ def rank_program(g, core, T, topo):
     def half(buf, o, w, n):
         return buf[64 * n:64 * n + 64, o + 2 * w:o + 3 * w], buf[64 - 64 * n:128 - 64 * n, o:o + w]
 
-    def order(t, s, e_s, lost):
-        ex, ar, thr, gg, yo, yb, sm = (T["%s%d" % (n, t)] for n in ("ex", "ar", "thr", "g", "yo", "yb", "sm"))
-        wait(A, e_s, e_fac)
-        e_ex = ev(A.activation(ex[:], T.ones[:, 0:32], AF.Abs, bias=TINY, scale=s))
-        wait(A, e_ex)
-        e_th = ev(A.activation(thr[:], T.fac[:], AF.Copy, scale=ex[:, 0:1]))
-        wait(V, e_s)
+    def order(t, so, e_s, lost, e_tab):
+        sr, ar, thr, gg, yo, yb, sm = (T["%s%d" % (n, t)] for n in ("sr", "ar", "thr", "g", "yo", "yb", "sm"))
         lost[0]()
-        wait(V, e_ex)
-        e_tp = ev(V.transpose(ar[:, 0:32], ex[:]))
+        wait(A, e_s, e_fac)
+        e_th = ev(A.activation(thr[:], T.fac[:], AF.Abs, scale=so[0]))
+        wait(V, e_s)
+        e_tp = ev(V.transpose(sr[:], so[1]))
         vw()
         lost[1]()
         wait(V, e_tp)
         wait(A, e_tp)
-        for n in range(4):
-            v(V.tensor_copy(*turn(ar, 0, 32, n, 1)))
-        v(V.tensor_copy(*half(ar, 0, 32, 0)))
-        v(V.tensor_copy(*half(ar, 0, 32, 1)))
-        for n in range(3):
-            a(A.activation(*turn(ar, 0, 32, n, 3), AF.Copy))
-        aw()
-        e_tn = ev(A.activation(*turn(ar, 0, 32, 3, 3), AF.Copy))
         vw()
-        wait(V, e_th, e_tn)
-        v(V.tensor_tensor(gg[:, 0:128], ar[:], thr[:], Op.is_gt))
+
+        def size(p0, p1, c, q0, q1):
+            v(tt(ar[p0:p1, c:c + 32], sr[q0:q1, 0:32], sr[q0:q1, 32:64], Op.max))
+        size(0, 128, 0, 0, 128)
+        size(0, 64, 64, 64, 128)
+        size(64, 128, 64, 0, 64)
+        for n in range(3):
+            size(32 * n, 32 * n + 32, 32, 32 * n + 32, 32 * n + 64)
+        for n in range(4):
+            m = (n + 3) % 4
+            a(A.activation(ar[32 * n:32 * n + 32, 96:128], sr[32 * m:32 * m + 32, 0:32], AF.Abs))
+        e_tn = ev(A.activation(ar[96:128, 32:64], sr[0:32, 0:32], AF.Abs))
         lost[2]()
         vw()
-        v(V.tensor_tensor_scan(yo[:], T.ones[:, 0:193], gg[:], 0.0, Op.mult, Op.add))
+        wait(V, e_th, e_tn)
+        V.wait_ge(T.sem.a, na[0])
+        v(tt(gg[:, 0:128], ar[:], thr[:], Op.is_gt))
+        lost[3]()
+        vw()
+        v(V.tensor_tensor_scan(yo[:], T.dz[:, 0:193], gg[:], 0.0, Op.mult, Op.add))
         vw()
         v(V.transpose(yb[:], yo[:, 129:193]))
         vw()
@@ -294,21 +298,21 @@ def rank_program(g, core, T, topo):
         v(V.tensor_copy(*half(sm, 8, 2, 0)))
         for n in range(4):
             a(A.activation(*turn(sm, 8, 2, n, 3), AF.Copy))
-        aw()
         e_zn = ev(A.activation(*half(sm, 8, 2, 1), AF.Copy))
         vw()
         wait(V, e_zn)
+        V.wait_ge(T.sem.a, na[0])
         v(V.tensor_reduce(sm[:, 16:17], sm[:, 8:16:2], X, Op.min))
         v(V.tensor_reduce(sm[:, 17:18], sm[:, 9:16:2], X, Op.min))
         vw()
         of = T["of%d" % t]
         e_of = ev(ts(of[:], sm[:, 16:18], 256.0, Op.mult))
-        wait(V, e_of)
-        wait(A, e_of)
-        tab, tabs, e_tab = (T.t0, T.t0s, [e_t0]) if t == 0 else (T.t1, T.t1s, e_t1)
+        tab, tabs = (T.t0, T.t0s) if t == 0 else (T.t1, T.t1s)
         sc, ss, la, ls = (T["%s%d" % (n, t)] for n in ("sc", "ss", "la", "ls"))
         wait(V, *e_tab)
         wait(A, *e_tab)
+        wait(V, e_of)
+        wait(A, e_of)
         e_sc = ev(V.tensor_copy(u32(sc[:]), u32(tab[:, 0:128]).indirect(of[:])))
         e_ss = ev(A.activation(ss[:], tabs[:, 0:128].indirect(of[:]), AF.Copy))
         sl = slice(NK * rank, NK * rank + NK)
@@ -323,26 +327,26 @@ def rank_program(g, core, T, topo):
             own.append(ev(SY.dma_start(u8(la[:, sl]), u8(sc[:, NK * i:NK * i + NK])), 16))
             wait(SY, e_ss)
             own.append(ev(SY.dma_start(ls[:, sl], ss[:, NK * i:NK * i + NK]), 16))
-        vr, vi, bsb = T["vr%d" % t], T["vi%d" % t], T["bsb%d" % t]
-        v(V.tensor_tensor(sm[:, 20:22], sm[:, 16:18], T.sel[:], Op.mult))
+        vx, vr, vi, bsb = T["vx%d" % t], T["vr%d" % t], T["vi%d" % t], T["bsb%d" % t]
+        for h in range(2):
+            v(ts(vx[:, 32 * h:32 * h + 32], T.ones[:, 0:32], sm[:, 16 + h:17 + h], Op.mult, 256.0, Op.mult))
         vw()
-        v(V.tensor_reduce(sm[:, 22:23], sm[:, 20:22], X, Op.add))
+        v(V.transpose(vx[:, 64:128], vx[:, 0:64]))
         vw()
-        v(ts(vr[:, 0:32], T.ones[:, 0:32], sm[:, 22:23], Op.mult))
-        vw()
-        v(V.transpose(vr[:, 32:64], vr[:, 0:32]))
-        vw()
-        v(ts(vr[:, 64:96], vr[:, 32:64], 256.0, Op.mult))
-        v(ts(vi[:, 0:32], vr[:, 32:64], 256.0, Op.mult))
-        v(ts(vi[:, 32:64], vr[:, 32:64], 256.0, Op.mult, float(t), Op.add))
+        for h in range(2):
+            s = vx[:, 64 + 32 * h:80 + 32 * h]
+            v(V.tensor_copy(vi[:, 16 * h:16 * h + 16], s))
+            if t:
+                v(ts(vi[:, 32 + 16 * h:48 + 16 * h], s, float(t), Op.add))
+            v(V.tensor_copy(vr[:, 16 * h:16 * h + 16], s))
         vw()
         v(V.tensor_copy(bsb[:, 0:32], vi[:, 0:32]))
-        v(ts(vi[:, 64:96], vi[:, 32:64], 7, Op.bitwise_and))
+        v(ts(vi[:, 64:96], vi[:, 32 * t:32 * t + 32], 7, Op.bitwise_and))
         vw()
-        v(V.tensor_tensor(vr[:, 96:128], vr[:, 64:96], bsb[:, 0:32], Op.subtract))
-        v(V.tensor_copy(vr[:, 128:160], vi[:, 64:96]))
+        v(tt(vr[:, 32:64], vr[:, 0:32], bsb[:, 0:32], Op.subtract))
+        v(V.tensor_copy(vr[:, 64:96], vi[:, 64:96]))
         vw()
-        e_b = ev(ts(bsb[:, 32:64], vr[:, 96:128], -32.0, Op.mult, 8.0, Op.add))
+        e_b = ev(ts(bsb[:, 32:64], vr[:, 32:64], -32.0, Op.mult, 8.0, Op.add))
         wait(SY, e_b)
         fin.append(ev(SY.dma_start(T.bs[2 * t:2 * t + 2, 0:32], bsb[0:1, 0:64]), 16))
         return own, e_b
@@ -350,46 +354,43 @@ def rank_program(g, core, T, topo):
     def rebuild_list(t, e_b):
         s = NK * REB[t].index(rank)
         vr, bsb, rl, ol = T["vr%d" % t], T["bsb%d" % t], T["rl%d" % t], T["ol%d" % t]
-        q, lost = vr[:, 128 + s:136 + s], bsb[:, 32 + s:40 + s]
-        v(ts(rl[:, 0:8], q, im1, Op.is_le, im1, Op.add))
-        v(ts(rl[:, 8:16], q, is0, Op.mult))
-        vw()
-        v(V.tensor_tensor(rl[:, 16:24], rl[:, 0:8], rl[:, 8:16], Op.max))
+        q, lost = vr[:, 64 + s:72 + s], bsb[:, 32 + s:40 + s]
+        v(ts(rl[:, 0:8], q, im1, Op.is_le, float(NK), Op.mult))
+        v(ts(rl[:, 8:16], q, im1, Op.is_le))
+        v(ts(rl[:, 16:24], q, is08, Op.mult))
         vw()
         wait(V, e_b)
-        v(V.tensor_tensor(rl[:, 24:32], rl[:, 16:24], lost, Op.is_equal))
-        v(ts(rl[:, 32:40], rl[:, 16:24], float(NK), Op.mult))
+        v(tt(rl[:, 24:32], lost, rl[:, 8:16], Op.subtract))
+        v(tt(rl[:, 32:40], rl[:, 0:8], T.kb[:], Op.add))
+        v(tt(rl[:, 40:48], rl[:, 16:24], T.rm[:], Op.add))
         vw()
-        v(ts(rl[:, 40:48], rl[:, 24:32], 64.0, Op.mult))
-        v(V.tensor_tensor(rl[:, 48:56], rl[:, 32:40], T.rr[:], Op.add))
+        v(ts(rl[:, 48:56:2], rl[:, 24:32:2], im1, Op.is_equal, lo64, Op.mult))
+        v(ts(rl[:, 49:56:2], rl[:, 25:32:2], im1, Op.is_equal, hi64, Op.mult))
+        v(tt(rl[:, 56:64], rl[:, 32:40], rl[:, 40:48], Op.max))
         vw()
-        v(V.tensor_tensor(rl[:, 56:64], rl[:, 40:48], rl[:, 48:56], Op.max))
+        v(tt(rl[:, 64:72], rl[:, 48:56], rl[:, 56:64], Op.max))
         vw()
-        v(ts(rl[:, 64:68], rl[:, 56:64:2], lo8, Op.mult))
-        v(ts(rl[:, 68:72], rl[:, 57:64:2], hi8, Op.mult))
+        v(tt(rl[:, 72:76], rl[:, 64:72:2], rl[:, 65:72:2], Op.max))
         vw()
-        v(V.tensor_tensor(rl[:, 72:76], rl[:, 64:68], rl[:, 68:72], Op.add))
-        vw()
-        e = ev(V.tensor_copy(ol[:], rl[:, 72:76]))
-        wait(V, e)
-        return e
+        return ev(V.tensor_copy(ol[:], rl[:, 72:76]))
 
-    def rebuild(t, own, e_ol):
+    def rebuild(t, own, e_ol, e_eq, e_free):
         la, ls, od, os_, h, nq, ns, sb, ol = (T["%s%d" % (n, t)] for n in ("la", "ls", "or", "os", "h", "nq", "ns", "sb", "ol"))
-        D = T.da if t == 0 else T.db
+        D, banks = (T.da, 4) if t == 0 else (T.db, 3)
         arr = (T.sem["s_la%d" % t], 7 * 2 * (EW // 4))
-        wait(V, *own)
+        wait(V, e_ol, e_eq, *own)
         wait(V, arr)
         e_oc = ev(V.tensor_copy(u32(od[:, 0:64]), u32(la[:, 0:96]).indirect(ol[:])))
         wait(A, e_ol, *own)
         wait(A, arr)
         e_os = ev(A.activation(os_[:, 0:64], ls[:, 0:96].indirect(ol[:]), AF.Copy))
+        wait(PE, *e_free)
         wait(PE, e_eq, e_oc, e_os)
         scans, cps = [], []
         for b in range(4):
-            k = 512 * (b % 3)
-            if b == 3:
-                wait(PE, scans[0])
+            k = 512 * (b % banks)
+            if b >= banks:
+                wait(PE, scans[b - banks])
             e_d = ev(PE.matmul_mx(D[:, k:k + 128], T.eq[:, 128 * b:128 * b + 128], T.eqs[:, 128 * b:128 * b + 128], od[:], os_[:], True, True))
             wait(V, e_d)
             scans.append(ev(V.tensor_tensor_scan(sb[:, 64 * b:64 * b + 64], T.d0[:], D[:, k:k + 64], 0.0, Op.mult, Op.subtract)))
@@ -410,20 +411,24 @@ def rank_program(g, core, T, topo):
         wait(SY, e_nq)
         return [ev(SY.dma_start(u8(tw[:, sl]), u8(nq[:, 0:NK])), 16), ev(SY.dma_start(tws[:, sl], ns[:, 0:NK]), 16)]
 
-    def table_list(t):
-        vr, ei, oi = T["vr%d" % t], T["ei%d" % t], T["oi%d" % t]
+    def table0(t):
         for c in range(8):
-            v(ts(ei[:, 32 * c:32 * c + 32], vr[:, 32:64], T.tgt[:, 8 * t + c:8 * t + c + 1], Op.is_equal))
-        vw()
-        v(V.tensor_tensor(ei[:, 256:512], ei[:, 0:256], T.kw[:], Op.mult))
-        vw()
+            v(ts(T["ei%d" % t][:, 32 * c:32 * c + 32], T["vr%d" % t][:, 0:32], T.tgt[:, 8 * t + c:8 * t + c + 1], Op.is_equal))
+
+    def table1(t):
+        ei = T["ei%d" % t]
+        v(tt(ei[:, 256:512], ei[:, 0:256], T.kw[:], Op.mult))
+
+    def table2(t):
+        ei = T["ei%d" % t]
         v(V.tensor_tensor_scan(ei[:, 512:768], T.seg[:], ei[:, 256:512], 0.0, Op.mult, Op.max))
-        vw()
-        v(V.tensor_tensor(ei[:, 768:776], ei[:, 543:768:32], T.src[:, 8 * t:8 * t + 8], Op.max))
-        vw()
-        e = ev(V.tensor_copy(oi[:], ei[:, 768:776]))
-        wait(V, e)
-        return e
+
+    def table3(t):
+        ei = T["ei%d" % t]
+        v(tt(ei[:, 768:776], ei[:, 543:768:32], T.src[:, 8 * t:8 * t + 8], Op.max))
+
+    def table4(t):
+        return ev(V.tensor_copy(T["oi%d" % t][:], T["ei%d" % t][:, 768:776]))
 
     def arrived(t):
         return (T.sem["s_nw%d" % t], EW * (6 if mine == t else 8))
@@ -433,139 +438,150 @@ def rank_program(g, core, T, topo):
     wait(A, s_ck)
     e_ag0 = ev(A.activation(T.ag[:, 0:8], T.ck[:, 2:64:8], AF.Abs))
     e_ag1 = ev(A.activation(T.ag[:, 8:16], T.ck[:, 4:64:8], AF.Abs))
+    vw()
     wait(V, s_ck)
     v(V.tensor_reduce(T.cf[:, 5:6], T.ck[:, 0:64:8], X, Op.add))
     vw()
-    e_s = ev(V.tensor_tensor_scan(T.so[:, 0:8], T.ones[:, 0:8], T.ck[:, 1:64:8], T.cf[:, 5:6], Op.mult, Op.subtract))
+    e_s = ev(V.tensor_tensor_scan(T.so[:], T.dz[:, 289:361], T.ck[:, 1:576:8], T.cf[:, 5:6], Op.mult, Op.subtract))
 
     def l0a():
         wait(V, e_ag0)
         v(V.tensor_reduce(T.cf[:, 6:7], T.ag[:, 0:8], X, Op.max))
-        vw()
-        v(ts(T.gt[:, 8:16], T.ag[:, 0:8], T.cf[:, 6:7], Op.is_equal))
 
     def l0b():
-        v(V.tensor_tensor(T.gt[:, 16:24], T.gt[:, 8:16], T.w0[:], Op.mult))
+        v(ts(T.gt[:, 8:16], T.ag[:, 0:8], T.cf[:, 6:7], Op.is_equal))
 
     def l0c():
+        v(tt(T.gt[:, 16:24], T.gt[:, 8:16], T.w0[:], Op.mult))
+
+    def l0d():
         v(V.tensor_reduce(T.g0[:, 129:130], T.gt[:, 16:24], X, Op.max))
 
-    own, e_b = order(0, T.so[:, 7:8], e_s, (l0a, l0b, l0c))
+    own, e_b = order(0, (T.so[:, 8:9], T.so[:, 8:72]), e_s, (l0a, l0b, l0c, l0d), [e_t0])
     new_own = []
     if mine == 0:
         e_ol = rebuild_list(0, e_b)
-        new_own = rebuild(0, own, e_ol)
+        e_eq = unpacker()
+        new_own = rebuild(0, own, e_ol, e_eq, [])
+    vr, bsb = T.vr0, T.bsb0
+    hit, hi = T.hit, T.hiti
     wait(V, e_b)
-    e_ur0, e_ur1, e_oz = late()
-    wait(A, e_uq, e_fac, e_ur0, e_ur1, e_oz)
-    e_us0 = ev(A.activation(T.urs[:, 0:128], T.uqs[:, 0:128].indirect(T.oz[:, 0:8]), AF.Copy))
-    e_us1 = ev(A.activation(T.urs[:, 128:256], T.uqs[:, 0:128].indirect(T.oz[:, 8:16]), AF.Copy))
-    codeq = T.cf[:, 4:5]
-    vr = T["vr0"]
     e_ms = []
     for r in range(N):
-        e_ms.append(ev(ts(T.msk[:, 32 * r:32 * r + 32], vr[:, 32:64], T.c1[:, r:r + 1], Op.is_equal, T.dm[:, r:r + 1], Op.mult)))
-    e_ms.append(ev(ts(T.msk[:, 256:288], vr[:, 32:64], codeq, Op.is_equal, -1.0, Op.mult)))
+        e_ms.append(ev(ts(T.msk[:, 32 * r:32 * r + 32], vr[:, 0:32], T.c1[:, 8 + r:9 + r], Op.is_equal, T.dm[:, r:r + 1], Op.mult)))
+    v(V.tensor_reduce(T.cf[:, 4:5], T.c1[:, 16:24], X, Op.add))
+    table0(0)
+    v(tt(hit[:, 0:32], bsb[:, 0:32], bsb[:, 32:64], Op.subtract))
+    v(tt(T.gt[:, 24:32], T.ck[:, 3:64:8], T.pm[:], Op.mult))
+    v(ts(hit[:, 32:64], bsb[:, 32:64], q1, Op.not_equal))
+    v(ts(hit[:, 160:192], vr[:, 32:64], 1.0 / 256, Op.mult))
+    vw()
+    e_ms.append(ev(ts(T.msk[:, 256:288], vr[:, 0:32], T.cf[:, 4:5], Op.is_equal, -1.0, Op.mult)))
     for r in range(N + 1):
         wait(A, e_ms[r])
-        if r:
-            aw()
-        a(A.activation(T.junk[:], T.msk[:, 32 * r:32 * r + 32], AF.Copy, accum_out=T.rep[:, r:r + 1]))
+        a(A.activation(T.junk[:, 32 * r:32 * r + 32], T.msk[:, 32 * r:32 * r + 32], AF.Copy, accum_out=T.rep[:, r:r + 1]))
     aw()
-    e_rep = ev(A.activation(T.gt[:, 64:72], T.rep[:, 0:8], AF.Copy))
-    e_oi = table_list(0)
-    wait(V, *e_ms)
-    hit, hi = T.hit, T.hiti
-    bsb = T["bsb0"]
-    v(V.tensor_tensor(hit[:, 0:32], bsb[:, 0:32], bsb[:, 32:64], Op.subtract))
-    v(V.tensor_tensor(T.gt[:, 24:32], T.ck[:, 3:64:8], T.pm[:], Op.mult))
-    v(ts(hit[:, 32:64], bsb[:, 32:64], q1, Op.not_equal))
-    vw()
+    e_rep = ev(A.activation(T.gt[:, 64:73], T.rep[:], AF.Copy))
     v(ts(hi[:, 0:32], hit[:, 0:32], 128.0, Op.add))
     v(V.tensor_reduce(T.cf[:, 7:8], T.gt[:, 24:32], X, Op.add))
-    wait(V, e_rep)
-    v(V.tensor_tensor(T.gt[:, 32:40], T.dm[:], T.gt[:, 64:72], Op.subtract))
-    v(ts(T.gt[:, 40:41], T.rep[:, 8:9], 1.0, Op.add, -1.0, Op.mult))
+    table1(0)
     vw()
     v(ts(hi[:, 32:64], hi[:, 0:32], 127, Op.bitwise_and))
-    v(V.tensor_tensor(T.xs[:, 65:297:33], T.ck[:, 3:64:8], T.gt[:, 32:40], Op.mult))
-    v(V.tensor_tensor(T.xs[:, 32:33], T.cf[:, 7:8], T.gt[:, 40:41], Op.mult))
-    v(V.tensor_tensor(T.w40[:, 0:8], T.gt[:, 32:40], T.wr[:], Op.mult))
-    wait(V, e_ag1)
-    v(V.tensor_tensor(T.gv[:, 0:8], T.gt[:, 32:40], T.ag[:, 8:16], Op.mult))
+    wait(V, e_seg)
+    table2(0)
     vw()
     v(V.tensor_copy(hit[:, 64:96], hi[:, 32:64]))
+    table3(0)
+    e_ur0 = ev(V.tensor_copy(u32(T.ur[:, 0:128]), u32(T.uq[:]).indirect(T.oz[:, 0:8])))
     vw()
+    e_oi = table4(0)
     v(ts(hit[:, 96:128], hit[:, 64:96], T.pf[:, 0:1], Op.is_equal))
+    wait(V, e_rep, *e_ms)
+    v(tt(T.gt[:, 32:40], T.dm[:], T.gt[:, 64:72], Op.subtract))
+    v(ts(T.gt[:, 40:41], T.gt[:, 72:73], 1.0, Op.add, -1.0, Op.mult))
     vw()
-    v(V.tensor_tensor(hit[:, 128:160], hit[:, 96:128], hit[:, 32:64], Op.mult))
+    v(tt(hit[:, 128:160], hit[:, 96:128], hit[:, 32:64], Op.mult))
+    v(tt(T.xs[:, 65:297:33], T.ck[:, 3:64:8], T.gt[:, 32:40], Op.mult))
+    v(tt(T.xs[:, 32:33], T.cf[:, 7:8], T.gt[:, 40:41], Op.mult))
+    v(tt(T.w40[:, 0:8], T.gt[:, 32:40], T.wr[:], Op.mult))
+    wait(V, e_ag1)
+    v(tt(T.gv[:, 0:8], T.gt[:, 32:40], T.ag[:, 8:16], Op.mult))
+    e_ur1 = ev(V.tensor_copy(u32(T.ur[:, 128:256]), u32(T.uq[:]).indirect(T.oz[:, 8:16])))
     vw()
-    v(V.tensor_tensor(hit[:, 0:32], hit[:, 128:160], vr[:, 96:128], Op.mult))
-    vw()
-    v(ts(T.w40[:, 8:40], hit[:, 0:32], 1.0 / 256, Op.mult))
-    vw()
+    v(tt(T.w40[:, 8:40], hit[:, 128:160], hit[:, 160:192], Op.mult))
+    wait(A, e_uq, e_oz, e_ur0, e_ur1)
+    e_us0 = ev(A.activation(T.urs[:, 0:128], T.uqs[:].indirect(T.oz[:, 0:8]), AF.Copy))
+    e_us1 = ev(A.activation(T.urs[:, 128:256], T.uqs[:].indirect(T.oz[:, 8:16]), AF.Copy))
+    wait(V, e_oi)
 
     nw = arrived(0)
     wait(PE, e_us0, e_us1, e_ur0, e_ur1)
     wait(PE, e_c0, e_c1, *new_own)
     wait(PE, nw)
-    e_cn = ev(PE.matmul_mx(T.ps[:, 0:128], T.ur[:, 0:128], T.urs[:, 0:128], T["tw0"][:, 128:256], T["tws0"][:, 128:256], True, True))
-    e_gn = ev(PE.matmul_mx(T.ps[:, 512:640], T.ur[:, 128:256], T.urs[:, 128:256], T["tw0"][:, 128:256], T["tws0"][:, 128:256], True, True))
+    e_cn = ev(PE.matmul_mx(T.ps[:, 0:128], T.ur[:, 0:128], T.urs[:, 0:128], T.tw0[:, 128:256], T.tws0[:, 128:256], True, True))
+    e_gn = ev(PE.matmul_mx(T.db[:, 0:128], T.ur[:, 128:256], T.urs[:, 128:256], T.tw0[:, 128:256], T.tws0[:, 128:256], True, True))
+    wait(V, *e_tw0)
     wait(V, *new_own)
-    wait(V, nw)
-    p1 = ev(V.tensor_copy(u32(T.t1[:]), u32(T["tw0"][:, 0:160]).indirect(T.oi0[:])))
-    wait(A, e_oi, *new_own)
-    wait(A, nw)
-    p2 = ev(A.activation(T.t1s[:], T["tws0"][:, 0:160].indirect(T.oi0[:]), AF.Copy))
-    e_t1 = [p1, p2]
-    wait(A, e_gn)
-    e_agn = ev(A.activation(T.agn[:], T.ps[:, 512:544], AF.Abs))
-    wait(SY, p1, p2)
-    e_tw = [ev(SY.dma_start(u8(T["tw1"][:, 0:128]), u8(T.t1[:])), 16), ev(SY.dma_start(T["tws1"][:, 0:128], T.t1s[:]), 16)]
-    wait(V, e_cn)
-    v(V.tensor_tensor(T.xs[:, 0:32], T.msk[:, 256:288], T.ps[:, 0:32], Op.mult))
-    for r in range(N - 1):
-        v(V.tensor_tensor(T.xs[:, 33 + 33 * r:65 + 33 * r], T.msk[:, 32 * r:32 * r + 32], T.ps[:, 0:32], Op.mult))
-    r = N - 1
-    e_xp = ev(V.tensor_tensor(T.xs[:, 33 + 33 * r:65 + 33 * r], T.msk[:, 32 * r:32 * r + 32], T.ps[:, 0:32], Op.mult))
     vw()
+    wait(V, nw)
+    p1 = ev(V.tensor_copy(u32(T.t1[:]), u32(T.tw0[:, 0:160]).indirect(T.oi0[:])))
+    wait(A, e_gn)
+    e_agn = ev(A.activation(T.agn[:], T.db[:, 0:32], AF.Abs))
+    wait(A, e_oi, *e_tw0)
+    wait(A, *new_own)
+    wait(A, nw)
+    p2 = ev(A.activation(T.t1s[:], T.tws0[:, 0:160].indirect(T.oi0[:]), AF.Copy))
+    wait(SY, p1, p2)
+    e_tw1 = [ev(SY.dma_start(u8(T.tw1[:, 0:128]), u8(T.t1[:])), 16), ev(SY.dma_start(T.tws1[:, 0:128], T.t1s[:]), 16)]
+    wait(V, e_cn)
+    for r in range(N):
+        v(tt(T.xs[:, 33 + 33 * r:65 + 33 * r], T.msk[:, 32 * r:32 * r + 32], T.ps[:, 0:32], Op.mult))
+    e_xp = ev(tt(T.xs[:, 0:32], T.msk[:, 256:288], T.ps[:, 0:32], Op.mult))
+    wait(V, e_agn)
+    v(tt(T.gv[:, 8:40], T.agn[:], hit[:, 128:160], Op.mult))
     wait(V, e_xp)
-    e_s = ev(V.tensor_tensor_scan(T.xo[:, 0:297], T.ones[:, 0:297], T.xs[:, 0:297], 0.0, Op.mult, Op.subtract))
+    vw()
+    e_s = ev(V.tensor_tensor_scan(T.xo[:], T.dz[:], T.xs[:], 0.0, Op.mult, Op.subtract))
 
     def l1a():
-        wait(V, e_agn)
-        v(V.tensor_tensor(T.gv[:, 8:40], T.agn[:], hit[:, 128:160], Op.mult))
-        vw()
         v(V.tensor_reduce(T.gt[:, 42:43], T.gv[:], X, Op.max))
 
     def l1b():
         v(ts(T.lw[:, 0:40], T.gv[:], T.gt[:, 42:43], Op.is_equal))
-        vw()
-        v(V.tensor_tensor(T.lw[:, 40:80], T.lw[:, 0:40], T.w40[:], Op.mult))
 
     def l1c():
+        v(tt(T.lw[:, 40:80], T.lw[:, 0:40], T.w40[:], Op.mult))
+
+    def l1d():
         v(V.tensor_reduce(T.g1[:, 129:130], T.lw[:, 40:80], X, Op.max))
 
-    own, e_b = order(1, T.xo[:, 296:297], e_s, (l1a, l1b, l1c))
+    own, e_b = order(1, (T.xo[:, 297:298], T.xo[:, 297:361]), e_s, (l1a, l1b, l1c, l1d), [p1, p2])
+    new_own = []
     if mine == 1:
         e_ol = rebuild_list(1, e_b)
         e_eq = unpacker()
-        new_own = rebuild(1, own, e_ol)
-    else:
-        new_own = []
+        new_own = rebuild(1, own, e_ol, e_eq, [e_agn])
     wait(V, e_b)
-    e_oi = table_list(1)
+    table0(1)
     wait(V, e_w, e_eb)
     e_wq = ev(V.quantize_mx(T.wq[:], T.wqs[:], T.wt[:]))
+    vw()
+    table1(1)
+    vw()
+    table2(1)
+    vw()
+    table3(1)
+    vw()
+    e_oi = table4(1)
     nw = arrived(1)
-    wait(V, *e_tw)
+    wait(V, e_oi, *e_tw1)
     wait(V, *new_own)
     wait(V, nw)
-    p1 = ev(V.tensor_copy(u32(T.t2[:]), u32(T["tw1"][:, 0:160]).indirect(T.oi1[:])))
-    wait(A, e_oi, *e_tw)
+    p1 = ev(V.tensor_copy(u32(T.t2[:]), u32(T.tw1[:, 0:160]).indirect(T.oi1[:])))
+    wait(A, e_oi, *e_tw1)
     wait(A, *new_own)
     wait(A, nw)
-    p2 = ev(A.activation(T.t2s[:], T["tws1"][:, 0:160].indirect(T.oi1[:]), AF.Copy))
+    p2 = ev(A.activation(T.t2s[:], T.tws1[:, 0:160].indirect(T.oi1[:]), AF.Copy))
     wait(SY, p1)
     fin.append(ev(SY.dma_start(T.oc[:, 0:512], u8(T.t2[:])), 16))
     wait(A, p2)

import numpy as np
from concourse.bass import DstId, RemoteDMATransfer
from concourse.mybir import dt, AluOpType as Op, AxisListType, ActivationFunctionType as AF

N, P, K = 8, 128, 32
REB = ((0, 2, 4, 6), (1, 3, 5, 7))
NK = K // 4
TINY = 2.0 ** -121
X4, U8, F32, I32, U16, BF = "float8_e4m3fn_x4", "uint8", "float32", "int32", "uint16", "bfloat16"


def _sb(n, d):
    return ("sbuf", [128, n], d)


SCRATCH = {
    "tbt": _sb(544, BF), "ut": _sb(512, BF), "wt": _sb(512, BF), "hz": _sb(512, BF), "eb": _sb(2048, BF),
    "t0": _sb(128, X4), "t0s": _sb(128, U8), "tr": _sb(128, X4), "trs": _sb(128, U8),
    "uq": _sb(128, X4), "uqs": _sb(128, U8), "wq": _sb(128, X4), "wqs": _sb(128, U8),
    "eq": _sb(512, X4), "eqs": _sb(512, U8),
    "ur": _sb(256, X4), "urs": _sb(256, U8),
    "t1": _sb(128, X4), "t1s": _sb(128, U8), "t2": _sb(128, X4), "t2s": _sb(128, U8),
    "ones": _sb(256, F32), "ident": _sb(128, F32), "ck": _sb(576, F32), "dz": _sb(361, F32),
    "pi": _sb(2, I32), "pj": _sb(4, I32), "cf": _sb(8, F32), "mk": _sb(4, F32), "rr": _sb(8, F32), "irow": _sb(32, F32),
    "pr": _sb(8, I32), "prb": _sb(8, I32), "xr": _sb(16, F32), "xi": _sb(16, I32), "xj": _sb(16, I32), "kw": _sb(256, F32), "pf": _sb(1, F32),
    "wr": _sb(8, F32), "w32": _sb(8, F32), "w0": _sb(8, F32), "dm": _sb(8, F32), "pm": _sb(8, F32), "c1": _sb(24, F32),
    "src": _sb(16, F32), "tgt": _sb(16, F32), "lc": _sb(8, F32), "rm": _sb(8, F32), "kb": _sb(8, F32), "fac": _sb(128, F32), "seg": _sb(256, F32),
    "d0": _sb(64, F32), "oz": _sb(16, U16),
    "ag": _sb(16, F32), "agn": _sb(32, F32), "so": _sb(72, F32), "xo": _sb(361, F32), "xs": _sb(361, F32), "msk": _sb(288, F32),
    "rep": _sb(9, F32), "junk": _sb(288, F32), "hit": _sb(192, F32), "hiti": _sb(64, I32), "gv": _sb(40, F32), "w40": _sb(40, F32), "gt": _sb(96, F32),
    "lw": _sb(96, F32), "ysb": _sb(128, F32),
    "ps": ("psum", [128, 512], F32), "da": ("psum", [128, 2048], F32), "db": ("psum", [128, 1536], F32),
}
for _t in "01":
    SCRATCH.update({
        "sc" + _t: _sb(32, X4), "ss" + _t: _sb(32, U8), "la" + _t: _sb(192, X4), "ls" + _t: _sb(192, U8),
        "or" + _t: _sb(128, X4), "os" + _t: _sb(128, U8), "h" + _t: _sb(512, BF), "nq" + _t: _sb(128, X4), "ns" + _t: _sb(128, U8),
        "tw" + _t: _sb(256, X4), "tws" + _t: _sb(256, U8), "sb" + _t: _sb(256, F32),
        "sr" + _t: _sb(64, F32), "ar" + _t: _sb(128, F32), "thr" + _t: _sb(128, F32), "g" + _t: _sb(193, F32), "yo" + _t: _sb(193, F32),
        "yb" + _t: _sb(64, F32), "sm" + _t: _sb(32, F32), "of" + _t: _sb(2, U16), "vx" + _t: _sb(128, F32), "vr" + _t: _sb(96, F32), "vi" + _t: _sb(96, I32),
        "bsb" + _t: _sb(64, F32), "rl" + _t: _sb(96, F32), "ol" + _t: _sb(4, U16), "ei" + _t: _sb(784, F32), "oi" + _t: _sb(8, U16),
    })
SEMAPHORES = ["v", "a", "sl", "s_ck", "s_la0", "s_la1", "s_nw0", "s_nw1"] + ["e%d" % _i for _i in range(135)]


def rank_program(g, core, T, topo):
    rank = T.rank_of(core)
    if rank is None:
        return
    V, A, PE, SY = g.vector, g.scalar, g.tensor, g.sync
    X = AxisListType.X
    used, nv, na, nsl, fin = [0], [0], [0], [0], []

    def ev(ins, n=1):
        s = T.sem["e%d" % used[0]]
        used[0] += 1
        ins.then_inc(s, n)
        return (s, n)

    def wait(q, *evs):
        for s, n in evs:
            q.wait_ge(s, n)

    def v(ins):
        ins.then_inc(T.sem.v, 1)
        nv[0] += 1

    def vw():
        V.wait_ge(T.sem.v, nv[0])

    def a(ins):
        ins.then_inc(T.sem.a, 1)
        na[0] += 1

    def aw():
        A.wait_ge(T.sem.a, na[0])

    def ts(out, i0, s1, op0, s2=None, op1=None):
        if op1 is None:
            return V.tensor_scalar(out, i0, s1, None, op0)
        return V.tensor_scalar(out, i0, s1, s2, op0, op1)

    def tt(out, i0, i1, op):
        return V.tensor_tensor(out, i0, i1, op)

    def u8(view):
        return view.bitcast(dt.uint8)

    def u32(view):
        return view.bitcast(dt.uint32)

    others = [r for r in range(N) if r != rank]
    EW = len(topo.engines(core, T.cores[others[0]]))

    def dst(r):
        rid, pid = topo.addr(T.cores[r], core)
        return DstId(rid=int(rid), pnc=int(pid))

    def to_all(src, out, sem):
        m = int(topo.mask(core, T.cores[others[0]]))
        g.remote_dma_fused([RemoteDMATransfer(dst_ids=[dst(r) for r in others], dma_engine_mask=m, remote_sem=sem, srcs=[src], dsts=[out for r in others])], local_sem=T.sem.sl)
        nsl[0] += EW

    def to_rebuilders(pairs, sem):
        tr = []
        for i, (r, s, d) in enumerate(pairs):
            es = topo.engines(core, T.cores[r])
            w = len(es) // 4
            m = 0
            for e in es[w * i:w * i + w]:
                m |= 1 << e
            tr.append(RemoteDMATransfer(dst_ids=[dst(r)], dma_engine_mask=m, remote_sem=sem, srcs=[s], dsts=[d]))
            nsl[0] += w
        g.remote_dma_fused(tr, local_sem=T.sem.sl)

    mine = [t for t in range(2) if rank in REB[t]][0]

    e_tb = ev(SY.dma_start(T.tbt[:, 0:512], T.tb[:, 0:512]), 16)
    e_tb2 = ev(A.dma_start(T.tbt[:, 512:544], T.tb[:, 0:32]), 16)
    e_u0 = ev(A.dma_start(T.ut[:, 0:4], T.u[:, 0:4]), 16)
    e_u1 = ev(A.dma_start(T.ut[:, 4:16], T.u[:, 0:12]), 16)

    def iota(out, pat, base, cm, f=True):
        if f:
            return ev(g.iota(out, pat, base, cm, allow_small_or_imprecise_dtypes=True))
        return ev(g.iota(out, pat, base, cm))
    i_pi = iota(T.pi[:, 0:2], [[1, 2]], 0, 1, False)
    i_rr = iota(T.rr[:, 0:8], [[1, 8]], 0, 0)
    i_ir = iota(T.irow[:, 0:32], [[1, 32]], 0, 0)
    i_pf = iota(T.pf[:, 0:1], [[0, 1]], 0, 1)
    i_pr = iota(T.pr[:, 0:8], [[1, 8]], 0, 1, False)
    i_x0 = iota(T.xr[:, 0:8], [[16, 8]], rank, 0)
    i_x1 = iota(T.xr[:, 8:16], [[16, 8]], P - rank, 0)

    v(V.memset(T.ut[:, 16:512], 0.0))
    e_hz = ev(V.memset(T.hz[:], 0.0))
    e_ones = ev(V.memset(T.ones[:], 1.0))
    wait(g, e_ones)
    e_id = ev(g.affine_select(T.ident[:], T.ones[:, 0:128], [[-1, 128]], Op.is_equal, 0.0, 0, 1))
    i_kw = iota(T.kw[:, 0:256], [[0, 8], [1, 32]], P, 0)
    wait(V, i_pi)
    v(ts(T.pj[:, 2:3], T.pi[:, 0:1], 7, Op.bitwise_and))
    v(ts(T.pj[:, 0:1], T.pi[:, 0:1], 15, Op.bitwise_and))
    v(ts(T.pj[:, 1:2], T.pi[:, 0:1], 31, Op.bitwise_and))
    v(ts(T.pj[:, 3:4], T.pi[:, 1:2], 7, Op.bitwise_and))
    vw()
    v(ts(T.mk[:, 0:1], T.pj[:, 2:3], float(rank), Op.is_equal))
    v(ts(T.mk[:, 1:2], T.pj[:, 2:3], float(rank), Op.not_equal))
    v(ts(T.mk[:, 2:3], T.pj[:, 2:3], float(rank), Op.not_equal))
    v(V.tensor_copy(T.cf[:, 0:4], T.pj[:, 0:4]))
    vw()
    p16, p32, p8, q1 = (T.cf[:, i:i + 1] for i in range(4))
    wait(V, e_u0, e_u1)
    e_uq = ev(V.quantize_mx(T.uq[:], T.uqs[:], T.ut[:]))
    wait(V, e_tb)
    e_t0 = ev(V.quantize_mx(T.t0[:], T.t0s[:], T.tbt[:, 0:512]))
    wait(V, e_tb2)
    e_tr = ev(V.quantize_mx(T.tr[:], T.trs[:], T.tbt[:, 4 * rank:4 * rank + 512]))
    wait(PE, e_uq, e_t0)
    e_m0 = ev(PE.matmul_mx(T.ps[:, 0:128], T.t0[:], T.t0s[:], T.uq[:], T.uqs[:], True, True))
    wait(PE, e_tr)
    e_m1 = ev(PE.matmul_mx(T.db[:, 0:128], T.tr[:], T.trs[:], T.uq[:], T.uqs[:], True, True))
    o = 8 * rank
    wait(V, e_m0)
    e_c0 = ev(tt(T.ck[:, o:o + 3], T.ps[:, 0:3], T.mk[:, 0:3], Op.mult))
    wait(V, e_m1)
    e_c1 = ev(V.tensor_copy(T.ck[:, o + 3:o + 5], T.db[:, 1:3]))
    wait(g, e_c0, e_c1)
    to_all(T.ck[:, o:o + 5], T.ck[:, o:o + 5], T.sem.s_ck)
    wait(SY, e_t0)
    e_tw0 = [ev(SY.dma_start(u8(T.tw0[:, 0:128]), u8(T.t0[:])), 16), ev(SY.dma_start(T.tws0[:, 0:128], T.t0s[:]), 16)]
    e_w = ev(SY.dma_start(T.wt[:], T.w[:, 0:512]), 16)

    wait(A, e_hz, e_ones)
    e_k0 = ev(A.activation(T.ck[:, 72:576], T.hz[:, 0:504], AF.Copy))
    e_k1 = ev(A.activation(T.dz[:, 0:256], T.ones[:], AF.Copy))
    e_k2 = ev(A.activation(T.dz[:, 256:361], T.ones[:, 0:105], AF.Copy))
    for b in range(4):
        a(A.activation(T.eb[:, 512 * b:512 * b + 512], T.hz[:], AF.Copy))
    e_k3 = ev(A.activation(T.d0[:], T.ones[:, 0:64], AF.Copy))
    wait(A, e_id)
    aw()
    for b in range(4):
        a(A.activation(T.eb[:, 512 * b + b:512 * b + 512:4], T.ident[:], AF.Copy))
    a(A.activation(T.seg[:], T.ones[:], AF.Copy))
    aw()
    e_seg = ev(A.activation(T.seg[:, 0:256:32], T.hz[:, 0:8], AF.Copy))
    e_eb = ev(A.activation(T["h%d" % mine][:], T.hz[:], AF.Copy))

    wait(V, e_hz, e_ones, e_uq, e_t0, e_tr, e_c0, e_c1)
    wait(V, i_rr, i_ir, i_pr, i_x0, i_x1, i_pf, i_kw)
    v(ts(T.fac[:, 0:32], T.irow[:], p32, Op.is_lt, -2.0 ** -24, Op.mult))
    v(V.memset(T.fac[:, 32:128], 1.0))
    v(V.memset(T.ck[:, 64:72], -TINY))
    v(V.memset(T.xs[:, 297:298], -TINY))
    v(V.memset(T.xs[:, 298:361], 0.0))
    v(V.memset(T.g0[:, 130:193], -1.0))
    v(V.memset(T.g1[:, 130:193], -1.0))
    v(ts(T.wr[:], T.rr[:], -1.0 / 8192, Op.mult, 8.0 / 8192, Op.add))
    v(ts(T.w32[:], T.rr[:], -1.0 / 32, Op.mult, 8.0 / 32, Op.add))
    v(ts(T.gt[:, 0:8], T.rr[:], p8, Op.not_equal))
    v(ts(T.prb[:], T.pr[:], 127, Op.bitwise_and))
    v(ts(T.xi[:], T.xr[:], p16, Op.add))
    v(ts(T.lc[:, 6:7], p16, 8.0, Op.is_ge, -1000.0, Op.mult))
    v(ts(T.lc[:, 7:8], p16, 8.0, Op.is_lt, -1000.0, Op.mult))
    v(ts(T.dm[:], T.rr[:], q1, Op.not_equal))
    v(ts(T.pm[:], T.rr[:], q1, Op.is_equal))
    vw()
    wait(V, e_k0, e_k1, e_k2)
    v(ts(T.fac[:, 0:32], T.fac[:, 0:32], 1.0, Op.add))
    for b in range(1, 4):
        v(V.memset(T.fac[32 * b:32 * b + 32, 128 - 32 * b:128], 1.0 - 2.0 ** -24))
    for gg in (T.g0, T.g1):
        v(V.memset(gg[:, 145:146], 15.0))
        v(V.memset(gg[:, 177:178], 15.0))
        v(ts(gg[:, 128:129], T.pf[:], 1.0 / 256, Op.mult))
    v(V.memset(T.dz[:, 329:330], -1.0))
    v(tt(T.w0[:], T.gt[:, 0:8], T.wr[:], Op.mult))
    v(ts(T.rm[:, 0:8:2], T.rr[:, 0:8:2], T.lc[:, 6:7], Op.add))
    v(ts(T.rm[:, 1:8:2], T.rr[:, 1:8:2], T.lc[:, 7:8], Op.add))
    v(ts(T.lc[:, 0:1], p8, -1.0, Op.add))
    v(ts(T.lc[:, 1:2], p8, 0.0, Op.is_equal, 8.0, Op.mult))
    v(ts(T.lc[:, 2:3], p16, 8.0, Op.is_lt, 64.0, Op.mult))
    v(ts(T.lc[:, 3:4], p16, 8.0, Op.is_ge, 64.0, Op.mult))
    v(ts(T.lc[:, 4:5], p8, -1.0, Op.add, 8.0, Op.mult))
    v(V.tensor_copy(T.c1[:, 0:8], T.prb[:]))
    v(ts(T.xj[:], T.xi[:], 127, Op.bitwise_and))
    v(V.memset(T.oz[:, 0:8], 0))
    v(V.memset(T.oz[:, 8:16], 2))
    e_fac = ev(V.quantize_mx(T.tw0[:, 128:256], T.tws0[:, 128:256], T.hz[:]))
    vw()
    wait(V, e_fac, e_k3)
    v(ts(T.kb[:], T.rm[:], T.lc[:, 4:5], Op.add))
    v(V.memset(T.d0[:, 0:64:8], 0.0))
    v(V.memset(T.d0[:, 1:64:8], -1.0))
    v(V.tensor_copy(T.src[:], T.xj[:]))
    e_oz = ev(tt(T.c1[:, 8:16], T.c1[:, 0:8], T.w32[:], Op.add))
    v(V.quantize_mx(T["la%d" % mine][:, 64:192], T["ls%d" % mine][:, 64:192], T.hz[:]))
    v(V.quantize_mx(T["or%d" % mine][:], T["os%d" % mine][:], T.hz[:]))
    vw()
    wait(V, e_oz)
    v(ts(T.tgt[:], T.src[:], (8 - rank) / 32.0, Op.add))
    v(tt(T.c1[:, 16:24], T.c1[:, 8:16], T.pm[:], Op.mult))
    im1, is08, lo64, hi64 = (T.lc[:, i:i + 1] for i in range(4))

    def unpacker():
        wait(V, e_eb)
        return ev(V.quantize_mx(T.eq[:], T.eqs[:], T.eb[:]))

    def turn(buf, o, w, n, k):
        m = (n + k) % 4
        return buf[32 * n:32 * n + 32, o + k * w:o + k * w + w], buf[32 * m:32 * m + 32, o:o + w]

    def half(buf, o, w, n):
        return buf[64 * n:64 * n + 64, o + 2 * w:o + 3 * w], buf[64 - 64 * n:128 - 64 * n, o:o + w]

    def order(t, so, e_s, lost, e_tab):
        sr, ar, thr, gg, yo, yb, sm = (T["%s%d" % (n, t)] for n in ("sr", "ar", "thr", "g", "yo", "yb", "sm"))
        lost[0]()
        wait(A, e_s, e_fac)
        e_th = ev(A.activation(thr[:], T.fac[:], AF.Abs, scale=so[0]))
        wait(V, e_s)
        e_tp = ev(V.transpose(sr[:], so[1]))
        vw()
        lost[1]()
        wait(V, e_tp)
        wait(A, e_tp)
        vw()

        def size(p0, p1, c, q0, q1):
            v(tt(ar[p0:p1, c:c + 32], sr[q0:q1, 0:32], sr[q0:q1, 32:64], Op.max))
        size(0, 128, 0, 0, 128)
        size(0, 64, 64, 64, 128)
        size(64, 128, 64, 0, 64)
        for n in range(3):
            size(32 * n, 32 * n + 32, 32, 32 * n + 32, 32 * n + 64)
        for n in range(4):
            m = (n + 3) % 4
            a(A.activation(ar[32 * n:32 * n + 32, 96:128], sr[32 * m:32 * m + 32, 0:32], AF.Abs))
        e_tn = ev(A.activation(ar[96:128, 32:64], sr[0:32, 0:32], AF.Abs))
        lost[2]()
        vw()
        wait(V, e_th, e_tn)
        V.wait_ge(T.sem.a, na[0])
        v(tt(gg[:, 0:128], ar[:], thr[:], Op.is_gt))
        lost[3]()
        vw()
        v(V.tensor_tensor_scan(yo[:], T.dz[:, 0:193], gg[:], 0.0, Op.mult, Op.add))
        vw()
        v(V.transpose(yb[:], yo[:, 129:193]))
        vw()
        e_z0 = ev(V.tensor_reduce(sm[:, 8:9], yb[:, 0:32], X, Op.min, apply_absolute_value=True))
        e_z1 = ev(V.tensor_reduce(sm[:, 9:10], yb[:, 32:64], X, Op.min, apply_absolute_value=True))
        wait(A, e_z0, e_z1)
        wait(V, e_z0, e_z1)
        for n in range(4):
            v(V.tensor_copy(*turn(sm, 8, 2, n, 1)))
        v(V.tensor_copy(*half(sm, 8, 2, 0)))
        for n in range(4):
            a(A.activation(*turn(sm, 8, 2, n, 3), AF.Copy))
        e_zn = ev(A.activation(*half(sm, 8, 2, 1), AF.Copy))
        vw()
        wait(V, e_zn)
        V.wait_ge(T.sem.a, na[0])
        v(V.tensor_reduce(sm[:, 16:17], sm[:, 8:16:2], X, Op.min))
        v(V.tensor_reduce(sm[:, 17:18], sm[:, 9:16:2], X, Op.min))
        vw()
        of = T["of%d" % t]
        e_of = ev(ts(of[:], sm[:, 16:18], 256.0, Op.mult))
        tab, tabs = (T.t0, T.t0s) if t == 0 else (T.t1, T.t1s)
        sc, ss, la, ls = (T["%s%d" % (n, t)] for n in ("sc", "ss", "la", "ls"))
        wait(V, *e_tab)
        wait(A, *e_tab)
        wait(V, e_of)
        wait(A, e_of)
        e_sc = ev(V.tensor_copy(u32(sc[:]), u32(tab[:, 0:128]).indirect(of[:])))
        e_ss = ev(A.activation(ss[:], tabs[:, 0:128].indirect(of[:]), AF.Copy))
        sl = slice(NK * rank, NK * rank + NK)
        wait(g, e_sc)
        to_rebuilders([(r, u8(sc[:, NK * i:NK * i + NK]), u8(la[:, sl])) for i, r in enumerate(REB[t]) if r != rank], T.sem["s_la%d" % t])
        wait(g, e_ss)
        to_rebuilders([(r, ss[:, NK * i:NK * i + NK], ls[:, sl]) for i, r in enumerate(REB[t]) if r != rank], T.sem["s_la%d" % t])
        own = []
        if rank in REB[t]:
            i = REB[t].index(rank)
            wait(SY, e_sc)
            own.append(ev(SY.dma_start(u8(la[:, sl]), u8(sc[:, NK * i:NK * i + NK])), 16))
            wait(SY, e_ss)
            own.append(ev(SY.dma_start(ls[:, sl], ss[:, NK * i:NK * i + NK]), 16))
        vx, vr, vi, bsb = T["vx%d" % t], T["vr%d" % t], T["vi%d" % t], T["bsb%d" % t]
        for h in range(2):
            v(ts(vx[:, 32 * h:32 * h + 32], T.ones[:, 0:32], sm[:, 16 + h:17 + h], Op.mult, 256.0, Op.mult))
        vw()
        v(V.transpose(vx[:, 64:128], vx[:, 0:64]))
        vw()
        for h in range(2):
            s = vx[:, 64 + 32 * h:80 + 32 * h]
            v(V.tensor_copy(vi[:, 16 * h:16 * h + 16], s))
            if t:
                v(ts(vi[:, 32 + 16 * h:48 + 16 * h], s, float(t), Op.add))
            v(V.tensor_copy(vr[:, 16 * h:16 * h + 16], s))
        vw()
        v(V.tensor_copy(bsb[:, 0:32], vi[:, 0:32]))
        v(ts(vi[:, 64:96], vi[:, 32 * t:32 * t + 32], 7, Op.bitwise_and))
        vw()
        v(tt(vr[:, 32:64], vr[:, 0:32], bsb[:, 0:32], Op.subtract))
        v(V.tensor_copy(vr[:, 64:96], vi[:, 64:96]))
        vw()
        e_b = ev(ts(bsb[:, 32:64], vr[:, 32:64], -32.0, Op.mult, 8.0, Op.add))
        wait(SY, e_b)
        fin.append(ev(SY.dma_start(T.bs[2 * t:2 * t + 2, 0:32], bsb[0:1, 0:64]), 16))
        return own, e_b

    def rebuild_list(t, e_b):
        s = NK * REB[t].index(rank)
        vr, bsb, rl, ol = T["vr%d" % t], T["bsb%d" % t], T["rl%d" % t], T["ol%d" % t]
        q, lost = vr[:, 64 + s:72 + s], bsb[:, 32 + s:40 + s]
        v(ts(rl[:, 0:8], q, im1, Op.is_le, float(NK), Op.mult))
        v(ts(rl[:, 8:16], q, im1, Op.is_le))
        v(ts(rl[:, 16:24], q, is08, Op.mult))
        vw()
        wait(V, e_b)
        v(tt(rl[:, 24:32], lost, rl[:, 8:16], Op.subtract))
        v(tt(rl[:, 32:40], rl[:, 0:8], T.kb[:], Op.add))
        v(tt(rl[:, 40:48], rl[:, 16:24], T.rm[:], Op.add))
        vw()
        v(ts(rl[:, 48:56:2], rl[:, 24:32:2], im1, Op.is_equal, lo64, Op.mult))
        v(ts(rl[:, 49:56:2], rl[:, 25:32:2], im1, Op.is_equal, hi64, Op.mult))
        v(tt(rl[:, 56:64], rl[:, 32:40], rl[:, 40:48], Op.max))
        vw()
        v(tt(rl[:, 64:72], rl[:, 48:56], rl[:, 56:64], Op.max))
        vw()
        v(tt(rl[:, 72:76], rl[:, 64:72:2], rl[:, 65:72:2], Op.max))
        vw()
        return ev(V.tensor_copy(ol[:], rl[:, 72:76]))

    def rebuild(t, own, e_ol, e_eq, e_free):
        la, ls, od, os_, h, nq, ns, sb, ol = (T["%s%d" % (n, t)] for n in ("la", "ls", "or", "os", "h", "nq", "ns", "sb", "ol"))
        D, banks = (T.da, 4) if t == 0 else (T.db, 3)
        arr = (T.sem["s_la%d" % t], 7 * 2 * (EW // 4))
        wait(V, e_ol, e_eq, *own)
        wait(V, arr)
        e_oc = ev(V.tensor_copy(u32(od[:, 0:64]), u32(la[:, 0:96]).indirect(ol[:])))
        wait(A, e_ol, *own)
        wait(A, arr)
        e_os = ev(A.activation(os_[:, 0:64], ls[:, 0:96].indirect(ol[:]), AF.Copy))
        wait(PE, *e_free)
        wait(PE, e_eq, e_oc, e_os)
        scans, cps = [], []
        for b in range(4):
            k = 512 * (b % banks)
            if b >= banks:
                wait(PE, scans[b - banks])
            e_d = ev(PE.matmul_mx(D[:, k:k + 128], T.eq[:, 128 * b:128 * b + 128], T.eqs[:, 128 * b:128 * b + 128], od[:], os_[:], True, True))
            wait(V, e_d)
            scans.append(ev(V.tensor_tensor_scan(sb[:, 64 * b:64 * b + 64], T.d0[:], D[:, k:k + 64], 0.0, Op.mult, Op.subtract)))
        for b in range(3):
            wait(A, scans[b])
            cps.append(ev(A.activation(h[:, b:4 * NK:4], sb[:, 64 * b + 7:64 * b + 64:8], AF.Copy)))
        wait(V, scans[3])
        cps.append(ev(V.tensor_copy(h[:, 3:4 * NK:4], sb[:, 199:256:8])))
        wait(V, e_eb, *scans)
        wait(V, *cps)
        e_nq = ev(V.quantize_mx(nq[:], ns[:], h[:]))
        i = REB[t].index(rank)
        sl = slice(P + NK * i, P + NK * i + NK)
        tw, tws = T["tw%d" % t], T["tws%d" % t]
        wait(g, e_nq)
        to_all(u8(nq[:, 0:NK]), u8(tw[:, sl]), T.sem["s_nw%d" % t])
        to_all(ns[:, 0:NK], tws[:, sl], T.sem["s_nw%d" % t])
        wait(SY, e_nq)
        return [ev(SY.dma_start(u8(tw[:, sl]), u8(nq[:, 0:NK])), 16), ev(SY.dma_start(tws[:, sl], ns[:, 0:NK]), 16)]

    def table0(t):
        for c in range(8):
            v(ts(T["ei%d" % t][:, 32 * c:32 * c + 32], T["vr%d" % t][:, 0:32], T.tgt[:, 8 * t + c:8 * t + c + 1], Op.is_equal))

    def table1(t):
        ei = T["ei%d" % t]
        v(tt(ei[:, 256:512], ei[:, 0:256], T.kw[:], Op.mult))

    def table2(t):
        ei = T["ei%d" % t]
        v(V.tensor_tensor_scan(ei[:, 512:768], T.seg[:], ei[:, 256:512], 0.0, Op.mult, Op.max))

    def table3(t):
        ei = T["ei%d" % t]
        v(tt(ei[:, 768:776], ei[:, 543:768:32], T.src[:, 8 * t:8 * t + 8], Op.max))

    def table4(t):
        return ev(V.tensor_copy(T["oi%d" % t][:], T["ei%d" % t][:, 768:776]))

    def arrived(t):
        return (T.sem["s_nw%d" % t], EW * (6 if mine == t else 8))

    s_ck = (T.sem.s_ck, 7 * EW)
    wait(A, e_c0, e_c1)
    wait(A, s_ck)
    e_ag0 = ev(A.activation(T.ag[:, 0:8], T.ck[:, 2:64:8], AF.Abs))
    e_ag1 = ev(A.activation(T.ag[:, 8:16], T.ck[:, 4:64:8], AF.Abs))
    vw()
    wait(V, s_ck)
    v(V.tensor_reduce(T.cf[:, 5:6], T.ck[:, 0:64:8], X, Op.add))
    vw()
    e_s = ev(V.tensor_tensor_scan(T.so[:], T.dz[:, 289:361], T.ck[:, 1:576:8], T.cf[:, 5:6], Op.mult, Op.subtract))

    def l0a():
        wait(V, e_ag0)
        v(V.tensor_reduce(T.cf[:, 6:7], T.ag[:, 0:8], X, Op.max))

    def l0b():
        v(ts(T.gt[:, 8:16], T.ag[:, 0:8], T.cf[:, 6:7], Op.is_equal))

    def l0c():
        v(tt(T.gt[:, 16:24], T.gt[:, 8:16], T.w0[:], Op.mult))

    def l0d():
        v(V.tensor_reduce(T.g0[:, 129:130], T.gt[:, 16:24], X, Op.max))

    own, e_b = order(0, (T.so[:, 8:9], T.so[:, 8:72]), e_s, (l0a, l0b, l0c, l0d), [e_t0])
    new_own = []
    if mine == 0:
        e_ol = rebuild_list(0, e_b)
        e_eq = unpacker()
        new_own = rebuild(0, own, e_ol, e_eq, [])
    vr, bsb = T.vr0, T.bsb0
    hit, hi = T.hit, T.hiti
    wait(V, e_b)
    e_ms = []
    for r in range(N):
        e_ms.append(ev(ts(T.msk[:, 32 * r:32 * r + 32], vr[:, 0:32], T.c1[:, 8 + r:9 + r], Op.is_equal, T.dm[:, r:r + 1], Op.mult)))
    v(V.tensor_reduce(T.cf[:, 4:5], T.c1[:, 16:24], X, Op.add))
    table0(0)
    v(tt(hit[:, 0:32], bsb[:, 0:32], bsb[:, 32:64], Op.subtract))
    v(tt(T.gt[:, 24:32], T.ck[:, 3:64:8], T.pm[:], Op.mult))
    v(ts(hit[:, 32:64], bsb[:, 32:64], q1, Op.not_equal))
    v(ts(hit[:, 160:192], vr[:, 32:64], 1.0 / 256, Op.mult))
    vw()
    e_ms.append(ev(ts(T.msk[:, 256:288], vr[:, 0:32], T.cf[:, 4:5], Op.is_equal, -1.0, Op.mult)))
    for r in range(N + 1):
        wait(A, e_ms[r])
        a(A.activation(T.junk[:, 32 * r:32 * r + 32], T.msk[:, 32 * r:32 * r + 32], AF.Copy, accum_out=T.rep[:, r:r + 1]))
    aw()
    e_rep = ev(A.activation(T.gt[:, 64:73], T.rep[:], AF.Copy))
    v(ts(hi[:, 0:32], hit[:, 0:32], 128.0, Op.add))
    v(V.tensor_reduce(T.cf[:, 7:8], T.gt[:, 24:32], X, Op.add))
    table1(0)
    vw()
    v(ts(hi[:, 32:64], hi[:, 0:32], 127, Op.bitwise_and))
    wait(V, e_seg)
    table2(0)
    vw()
    v(V.tensor_copy(hit[:, 64:96], hi[:, 32:64]))
    table3(0)
    e_ur0 = ev(V.tensor_copy(u32(T.ur[:, 0:128]), u32(T.uq[:]).indirect(T.oz[:, 0:8])))
    vw()
    e_oi = table4(0)
    v(ts(hit[:, 96:128], hit[:, 64:96], T.pf[:, 0:1], Op.is_equal))
    wait(V, e_rep, *e_ms)
    v(tt(T.gt[:, 32:40], T.dm[:], T.gt[:, 64:72], Op.subtract))
    v(ts(T.gt[:, 40:41], T.gt[:, 72:73], 1.0, Op.add, -1.0, Op.mult))
    vw()
    v(tt(hit[:, 128:160], hit[:, 96:128], hit[:, 32:64], Op.mult))
    v(tt(T.xs[:, 65:297:33], T.ck[:, 3:64:8], T.gt[:, 32:40], Op.mult))
    v(tt(T.xs[:, 32:33], T.cf[:, 7:8], T.gt[:, 40:41], Op.mult))
    v(tt(T.w40[:, 0:8], T.gt[:, 32:40], T.wr[:], Op.mult))
    wait(V, e_ag1)
    v(tt(T.gv[:, 0:8], T.gt[:, 32:40], T.ag[:, 8:16], Op.mult))
    e_ur1 = ev(V.tensor_copy(u32(T.ur[:, 128:256]), u32(T.uq[:]).indirect(T.oz[:, 8:16])))
    vw()
    v(tt(T.w40[:, 8:40], hit[:, 128:160], hit[:, 160:192], Op.mult))
    wait(A, e_uq, e_oz, e_ur0, e_ur1)
    e_us0 = ev(A.activation(T.urs[:, 0:128], T.uqs[:].indirect(T.oz[:, 0:8]), AF.Copy))
    e_us1 = ev(A.activation(T.urs[:, 128:256], T.uqs[:].indirect(T.oz[:, 8:16]), AF.Copy))
    wait(V, e_oi)

    nw = arrived(0)
    wait(PE, e_us0, e_us1, e_ur0, e_ur1)
    wait(PE, e_c0, e_c1, *new_own)
    wait(PE, nw)
    e_cn = ev(PE.matmul_mx(T.ps[:, 0:128], T.ur[:, 0:128], T.urs[:, 0:128], T.tw0[:, 128:256], T.tws0[:, 128:256], True, True))
    e_gn = ev(PE.matmul_mx(T.db[:, 0:128], T.ur[:, 128:256], T.urs[:, 128:256], T.tw0[:, 128:256], T.tws0[:, 128:256], True, True))
    wait(V, *e_tw0)
    wait(V, *new_own)
    vw()
    wait(V, nw)
    p1 = ev(V.tensor_copy(u32(T.t1[:]), u32(T.tw0[:, 0:160]).indirect(T.oi0[:])))
    wait(A, e_gn)
    e_agn = ev(A.activation(T.agn[:], T.db[:, 0:32], AF.Abs))
    wait(A, e_oi, *e_tw0)
    wait(A, *new_own)
    wait(A, nw)
    p2 = ev(A.activation(T.t1s[:], T.tws0[:, 0:160].indirect(T.oi0[:]), AF.Copy))
    wait(SY, p1, p2)
    e_tw1 = [ev(SY.dma_start(u8(T.tw1[:, 0:128]), u8(T.t1[:])), 16), ev(SY.dma_start(T.tws1[:, 0:128], T.t1s[:]), 16)]
    wait(V, e_cn)
    for r in range(N):
        v(tt(T.xs[:, 33 + 33 * r:65 + 33 * r], T.msk[:, 32 * r:32 * r + 32], T.ps[:, 0:32], Op.mult))
    e_xp = ev(tt(T.xs[:, 0:32], T.msk[:, 256:288], T.ps[:, 0:32], Op.mult))
    wait(V, e_agn)
    v(tt(T.gv[:, 8:40], T.agn[:], hit[:, 128:160], Op.mult))
    wait(V, e_xp)
    vw()
    e_s = ev(V.tensor_tensor_scan(T.xo[:], T.dz[:], T.xs[:], 0.0, Op.mult, Op.subtract))

    def l1a():
        v(V.tensor_reduce(T.gt[:, 42:43], T.gv[:], X, Op.max))

    def l1b():
        v(ts(T.lw[:, 0:40], T.gv[:], T.gt[:, 42:43], Op.is_equal))

    def l1c():
        v(tt(T.lw[:, 40:80], T.lw[:, 0:40], T.w40[:], Op.mult))

    def l1d():
        v(V.tensor_reduce(T.g1[:, 129:130], T.lw[:, 40:80], X, Op.max))

    own, e_b = order(1, (T.xo[:, 297:298], T.xo[:, 297:361]), e_s, (l1a, l1b, l1c, l1d), [p1, p2])
    new_own = []
    if mine == 1:
        e_ol = rebuild_list(1, e_b)
        e_eq = unpacker()
        new_own = rebuild(1, own, e_ol, e_eq, [e_agn])
    wait(V, e_b)
    table0(1)
    wait(V, e_w, e_eb)
    e_wq = ev(V.quantize_mx(T.wq[:], T.wqs[:], T.wt[:]))
    vw()
    table1(1)
    vw()
    table2(1)
    vw()
    table3(1)
    vw()
    e_oi = table4(1)
    nw = arrived(1)
    wait(V, e_oi, *e_tw1)
    wait(V, *new_own)
    wait(V, nw)
    p1 = ev(V.tensor_copy(u32(T.t2[:]), u32(T.tw1[:, 0:160]).indirect(T.oi1[:])))
    wait(A, e_oi, *e_tw1)
    wait(A, *new_own)
    wait(A, nw)
    p2 = ev(A.activation(T.t2s[:], T.tws1[:, 0:160].indirect(T.oi1[:]), AF.Copy))
    wait(SY, p1)
    fin.append(ev(SY.dma_start(T.oc[:, 0:512], u8(T.t2[:])), 16))
    wait(A, p2)
    for k in range(4):
        fin.append(ev(A.dma_start(T.osc[4 * k:4 * k + 4, 0:128], T.t2s[32 * k:32 * k + 4, 0:128]), 16))
    wait(PE, e_wq, e_xp, p1, p2)
    e_y = ev(PE.matmul_mx(T.ps[:, 0:128], T.wq[:], T.wqs[:], T.t2[:], T.t2s[:], True, True))
    wait(V, e_y)
    e_yc = ev(V.tensor_copy(T.ysb[:], T.ps[:, 0:128]))
    wait(SY, e_yc)
    fin.append(ev(SY.dma_start(T.y[:, 0:128], T.ysb[:]), 16))
    wait(g, *fin)
    g.wait_ge(T.sem.sl, nsl[0])
